import numpy as np
import ml_dtypes


def mxq(x, axis, fmt="e4m3"):
    dtype, down = {"e4m3": (ml_dtypes.float8_e4m3fn, 7), "e5m2": (ml_dtypes.float8_e5m2, 14)}[fmt]
    v = np.moveaxis(np.asarray(x, np.float32).astype(ml_dtypes.bfloat16).astype(np.float64), axis, -1)
    blocks = v.reshape(v.shape[:-1] + (-1, 32))
    amax = np.abs(blocks).max(-1, keepdims=True)
    byte = np.maximum(np.where(amax > 0, np.frexp(amax)[1] - 1 + 127, 0) - down, 1)
    scale = np.exp2(byte - 127.0)
    codes = (blocks / scale).astype(np.float32).astype(dtype).astype(np.float64)
    return np.moveaxis((codes * scale).reshape(v.shape), -1, axis)


WIDE = False


def mx_kscale(k):
    if not WIDE:
        return np.ones(k)
    levels = np.array([10, -10, 5, -5, 0])
    if k % 512:
        return np.exp2(np.random.permutation(np.resize(levels, k // 32))).repeat(32)
    a = np.empty((k // 512, 16))
    for p in range(k // 512):
        a[p, :8] = np.random.permutation(np.resize(levels, 8))
        for g in range(8):
            far = levels[np.abs(levels - a[p, g]) >= 10]
            a[p, g + 8] = far[np.random.randint(len(far))]
    return np.exp2(a.ravel()).repeat(32)


def f64(x):
    return np.asarray(x).astype(np.float64)


def striped(idx):
    return np.tile(idx.reshape(-1, 16).T, (8, 1)).astype(np.uint16)


def unstriped(offs):
    return offs[:16].T.reshape(-1).astype(np.int64)


def pack_weight(w):
    k, n = w.shape
    w = f64(np.asarray(w, np.float32).astype(ml_dtypes.bfloat16)).reshape(k // 32, 32, n)
    amax = np.abs(w).max(1)
    byte = np.clip(np.where(amax > 0, np.frexp(amax)[1] - 1 + 127 - 7, 1), 1, 254)
    scaled = (w * np.exp2(127.0 - byte)[:, None, :]).reshape(k, n).astype(np.float32)
    words = np.ascontiguousarray(scaled.reshape(k // 512, 128, 4, n).transpose(0, 1, 3, 2)).astype(ml_dtypes.float8_e4m3fn).view(np.uint8)
    return words, np.ascontiguousarray(byte.astype(np.uint8).reshape(k // 512, 16, n))


def unpack_weight(words, scales):
    g, p, n, _ = words.shape
    vals = np.ascontiguousarray(words).view(ml_dtypes.float8_e4m3fn).astype(np.float64) * np.repeat(np.exp2(scales.astype(np.float64) - 127.0), 8, axis=1)[..., None]
    return vals.transpose(0, 1, 3, 2).reshape(g * 512, n)


K, T, S, N, D, U = 512, 2048, 512, 256, 3, 1024
P = 2 ** 7


def setup_inputs():
    n = np.random.standard_normal
    s = mx_kscale(K)[:, None]
    packed_xT = pack_weight(n((K, T)) * s)
    return {
        "x_words": packed_xT[0],
        "x_scales": packed_xT[1],
        "w1": (n((K, N)) / np.sqrt(K) / s).astype(np.float32),
        "alpha": (n((N, U))).astype(np.float32),
        "trans": (np.tile(0.7 * n((D, 1, S)), (1, P, 1))).astype(np.float32),
        "offs": striped(np.random.permutation(T)[:S]),
        "pos1": striped(np.random.permutation(U)[:S]),
        "pos2": striped(np.random.permutation(U)[:S]),
        "pos3": striped(np.random.permutation(U)[:S]),
    }


def reference(x_words, x_scales, w1, alpha, trans, offs, pos1, pos2, pos3):
    a0 = f64(alpha)[:, unstriped(pos1)] + f64(trans)[0, :1]
    a1 = f64(alpha)[:, unstriped(pos2)] + f64(trans)[1, :1]
    a2 = f64(alpha)[:, unstriped(pos3)] + f64(trans)[2, :1]
    xq = unpack_weight(x_words, x_scales)[:, unstriped(offs)]
    y = mxq(f64(w1), 0, "e4m3").T @ xq
    return np.maximum(np.maximum(a0, a1), a2) + y

@@ -1,0 +1,85 @@
+from contextlib import ExitStack
+
+import concourse.mybir as mybir
+
+K, T, S, N, D, U = 512, 2048, 512, 256, 3, 1024
+P = 128
+PACK = 4
+FLOPS = 2 * K * N * S
+
+F32 = mybir.dt.float32
+BF16 = mybir.dt.bfloat16
+I32 = mybir.dt.int32
+U32 = mybir.dt.uint32
+U16 = mybir.dt.uint16
+U8 = mybir.dt.uint8
+FP8X4 = mybir.dt.float8_e4m3fn_x4
+ADD = mybir.AluOpType.add
+MAX = mybir.AluOpType.max
+
+
+def tile_picked_ycrf_vit_p_kernel(tc, x_words, x_scales, w1, alpha, trans, offs, pos1, pos2, pos3, out):
+    nc = tc.nc
+    with ExitStack() as ctx:
+        keep = ctx.enter_context(tc.tile_pool(name="keep", bufs=1))
+        psum = ctx.enter_context(tc.psum_pool(name="psum", bufs=1))
+
+        pos = [keep.tile([P, S // 16], U16, name=f"pos{d}") for d in range(D)]
+        picks = keep.tile([P, S // 16], U16, name="picks")
+        rows = [keep.tile([P, U], F32, name=f"alpha{h}") for h in range(2)]
+        tr = [keep.tile([P, S], F32, name=f"trans{d}") for d in range(D)]
+        words = keep.tile([P, T], I32, name="words", align_bytes=64)
+        scales = keep.tile([P, T], U8, name="scales", align_bytes=64)
+        w_raw = keep.tile([P, PACK, N], F32, name="w_raw")
+        w_bf = keep.tile([P, N, PACK], BF16, name="w_bf", align_bytes=64)
+        w_codes = keep.tile([P, N], U32, name="w_codes", align_bytes=64)
+        w_scales = keep.tile([P, N], U8, name="w_scales", align_bytes=64)
+        x_codes = keep.tile([P, S], U32, name="x_codes", align_bytes=64)
+        x_sc = keep.tile([P, S], U8, name="x_sc", align_bytes=64)
+
+        nc.vector.memset(scales[:].bitcast(I32), 0)
+
+        nc.sync.dma_start(pos[0][:], pos1)
+        nc.sync.dma_start(rows[0][:], alpha[0:P, :])
+        nc.sync.dma_start(tr[0][:], trans[0])
+        nc.sync.dma_start(pos[1][:], pos2)
+        nc.sync.dma_start(tr[1][:], trans[1])
+        nc.sync.dma_start(pos[2][:], pos3)
+        nc.sync.dma_start(tr[2][:], trans[2])
+        nc.sync.dma_start(picks[:], offs)
+        for q in range(4):
+            nc.sync.dma_start(scales[32 * q : 32 * q + 4, :].bitcast(I32), x_scales[0, 4 * q : 4 * q + 4, :].bitcast(I32))
+        nc.sync.dma_start(words[:], x_words[0].rearrange("p n t -> p (n t)").bitcast(I32))
+        nc.sync.dma_start(w_raw[:], w1.rearrange("(p j) n -> p j n", j=PACK))
+        nc.sync.dma_start(rows[1][:], alpha[P : 2 * P, :])
+
+        cand = [[keep.tile([P, S], F32, name=f"cand{h}{d}") for d in range(D)] for h in range(2)]
+        m2 = [keep.tile([P, S], F32, name=f"m2{h}") for h in range(2)]
+        m3 = [keep.tile([P, S], F32, name=f"m3{h}") for h in range(2)]
+        res = [keep.tile([P, S], F32, name=f"res{h}") for h in range(2)]
+        y = [psum.tile([P, S], F32, name=f"y{h}") for h in range(2)]
+
+        def look_up(h, d):
+            nc.vector.tensor_tensor(cand[h][d][:], rows[h][:].indirect(pos[d][:]), tr[d][:], ADD)
+
+        for d in range(D):
+            look_up(0, d)
+        nc.vector.tensor_tensor(m2[0][:], cand[0][0][:], cand[0][1][:], MAX)
+        nc.vector.tensor_copy(x_sc[:], scales[:].indirect(picks[:]))
+        nc.vector.tensor_tensor(m3[0][:], m2[0][:], cand[0][2][:], MAX)
+        nc.vector.tensor_copy(x_codes[:], words[:].bitcast(U32).indirect(picks[:]))
+        nc.scalar.copy(w_bf[:], w_raw[:].rearrange("p j n -> p n j"))
+        nc.vector.quantize_mx(out=w_codes[:].bitcast(FP8X4), scales=w_scales[:], in_=w_bf[:].rearrange("p n j -> p (n j)"))
+        for h in range(2):
+            cols = slice(h * P, (h + 1) * P)
+            nc.tensor.matmul_mx(out=y[h][:], lhsT=w_codes[:, cols].bitcast(FP8X4), lhsT_scale=w_scales[:, cols],
+                                rhs=x_codes[:].bitcast(FP8X4), rhs_scale=x_sc[:], start=True, stop=True)
+        look_up(1, 0)
+        look_up(1, 1)
+        nc.vector.tensor_tensor(res[0][:], y[0][:], m3[0][:], ADD)
+        nc.sync.dma_start(out[0:P, :], res[0][:])
+        nc.vector.tensor_tensor(m2[1][:], cand[1][0][:], cand[1][1][:], MAX)
+        look_up(1, 2)
+        nc.vector.tensor_tensor(m3[1][:], m2[1][:], cand[1][2][:], MAX)
+        nc.vector.tensor_tensor(res[1][:], y[1][:], m3[1][:], ADD)
+        nc.sync.dma_start(out[P : 2 * P, :], res[1][:])

@@ -1,6 +1,7 @@
 from contextlib import ExitStack
 
 import concourse.mybir as mybir
+from concourse.masks import make_identity
 
 K, T, S, N, D, U = 512, 2048, 512, 256, 3, 1024
 P = 128
@@ -16,6 +17,10 @@ U8 = mybir.dt.uint8
 FP8X4 = mybir.dt.float8_e4m3fn_x4
 ADD = mybir.AluOpType.add
 MAX = mybir.AluOpType.max
+IDENTITY = mybir.ActivationFunctionType.Identity
+B = S // P
+H = N // P
+QUAD = 32
 
 
 def tile_picked_ycrf_vit_p_kernel(tc, x_words, x_scales, w1, alpha, trans, offs, pos1, pos2, pos3, out):
@@ -26,9 +31,8 @@ def tile_picked_ycrf_vit_p_kernel(tc, x_words, x_scales, w1, alpha, trans, offs,
 
         pos = [keep.tile([P, S // 16], U16, name=f"pos{d}") for d in range(D)]
         picks = keep.tile([P, S // 16], U16, name="picks")
-        rows = [keep.tile([P, U], F32, name=f"alpha{h}") for h in range(2)]
-        tr = [keep.tile([P, S], F32, name=f"trans{d}") for d in range(D)]
-        words = keep.tile([P, T], I32, name="words", align_bytes=64)
+        rows = [keep.tile([P, U], F32, name=f"alpha{h}") for h in range(H)]
+        words = keep.tile([P, T], I32, name="words")
         scales = keep.tile([P, T], U8, name="scales", align_bytes=64)
         w_raw = keep.tile([P, PACK, N], F32, name="w_raw")
         w_bf = keep.tile([P, N, PACK], BF16, name="w_bf", align_bytes=64)
@@ -36,50 +40,120 @@ def tile_picked_ycrf_vit_p_kernel(tc, x_words, x_scales, w1, alpha, trans, offs,
         w_scales = keep.tile([P, N], U8, name="w_scales", align_bytes=64)
         x_codes = keep.tile([P, S], U32, name="x_codes", align_bytes=64)
         x_sc = keep.tile([P, S], U8, name="x_sc", align_bytes=64)
+        ident = keep.tile([P, P], F32, name="ident")
+        t_rows = keep.tile([P, D, P], F32, name="t_rows")
+        t_cols = keep.tile([P, D, B], F32, name="t_cols")
 
+        nc.gpsimd.memset(t_rows[:], 0.0)
         nc.vector.memset(scales[:].bitcast(I32), 0)
+        make_identity(nc, ident[:])
 
         nc.sync.dma_start(pos[0][:], pos1)
         nc.sync.dma_start(rows[0][:], alpha[0:P, :])
-        nc.sync.dma_start(tr[0][:], trans[0])
         nc.sync.dma_start(pos[1][:], pos2)
-        nc.sync.dma_start(tr[1][:], trans[1])
+        nc.sync.dma_start(t_rows[0:B, :, :], trans[:, 0, :].rearrange("d (b j) -> b d j", b=B))
         nc.sync.dma_start(pos[2][:], pos3)
-        nc.sync.dma_start(tr[2][:], trans[2])
-        nc.sync.dma_start(picks[:], offs)
-        for q in range(4):
-            nc.sync.dma_start(scales[32 * q : 32 * q + 4, :].bitcast(I32), x_scales[0, 4 * q : 4 * q + 4, :].bitcast(I32))
-        nc.sync.dma_start(words[:], x_words[0].rearrange("p n t -> p (n t)").bitcast(I32))
         nc.sync.dma_start(w_raw[:], w1.rearrange("(p j) n -> p j n", j=PACK))
+        nc.sync.dma_start(picks[:], offs)
+        nc.sync.dma_start(words[:], x_words[0].rearrange("p n t -> p (n t)").bitcast(I32))
+        for q in range(4):
+            nc.sync.dma_start(scales[QUAD * q : QUAD * q + 4, :].bitcast(I32), x_scales[0, 4 * q : 4 * q + 4, :].bitcast(I32))
         nc.sync.dma_start(rows[1][:], alpha[P : 2 * P, :])
 
-        cand = [[keep.tile([P, S], F32, name=f"cand{h}{d}") for d in range(D)] for h in range(2)]
-        m2 = [keep.tile([P, S], F32, name=f"m2{h}") for h in range(2)]
-        m3 = [keep.tile([P, S], F32, name=f"m3{h}") for h in range(2)]
-        res = [keep.tile([P, S], F32, name=f"res{h}") for h in range(2)]
-        y = [psum.tile([P, S], F32, name=f"y{h}") for h in range(2)]
+        def turn(bank, src, first, last):
+            for b in range(B):
+                nc.tensor.matmul(bank[:, b, :], src(b), ident[:], start=(first and b == 0), stop=(last and b == B - 1), is_transpose=True)
 
-        def look_up(h, d):
-            nc.vector.tensor_tensor(cand[h][d][:], rows[h][:].indirect(pos[d][:]), tr[d][:], ADD)
-
+        t_bank = psum.tile([P, B, P], F32, name="t_bank", tag="sum")
         for d in range(D):
-            look_up(0, d)
-        nc.vector.tensor_tensor(m2[0][:], cand[0][0][:], cand[0][1][:], MAX)
-        nc.vector.tensor_copy(x_sc[:], scales[:].indirect(picks[:]))
-        nc.vector.tensor_tensor(m3[0][:], m2[0][:], cand[0][2][:], MAX)
-        nc.vector.tensor_copy(x_codes[:], words[:].bitcast(U32).indirect(picks[:]))
-        nc.scalar.copy(w_bf[:], w_raw[:].rearrange("p j n -> p n j"))
-        nc.vector.quantize_mx(out=w_codes[:].bitcast(FP8X4), scales=w_scales[:], in_=w_bf[:].rearrange("p n j -> p (n j)"))
-        for h in range(2):
+            nc.tensor.transpose(t_bank[:, d, :], t_rows[:, d, :], ident[:])
+        nc.scalar.copy(t_cols[:], t_bank[:, 0:D, 0:B])
+
+        def spread(bank, d, last):
+            turn(bank, lambda b: t_cols[:, d, b : b + 1].to_broadcast([P, P]), True, last)
+
+        def flat(tile):
+            return tile[:].rearrange("p b j -> p (b j)")
+
+        t1_bank = psum.tile([P, B, P], F32, name="t1_bank")
+        t1_wide = keep.tile([P, B, P], F32, name="t1_wide")
+        y_t = [keep.tile([P, B, P], F32, name=f"y_t{h}") for h in range(H)]
+        y_last = keep.tile([P, S], F32, name="y_last")
+        res = [keep.tile([P, S], F32, name=f"res{h}") for h in range(H)]
+
+        def pick(h, d):
+            picked = keep.tile([P, B, P], F32, name=f"picked{h}{d}", tag=f"picked{h}{d}")
+            nc.vector.tensor_copy(flat(picked), rows[h][:].indirect(pos[d][:]))
+            return picked
+
+        def scores_by_bias(h, d, picked):
+            bank = psum.tile([P, B, P], F32, name=f"turned{h}{d}", tag=f"turned{d}")
+            scores = keep.tile([P, B, P], F32, name=f"scores{h}{d}", tag=f"scores{h}{d}")
+            for b in range(B):
+                nc.tensor.transpose(bank[:, b, :], picked[:, b, :], ident[:])
+            for b in range(B):
+                nc.scalar.activation(scores[:, b, :], bank[:, b, :], IDENTITY, bias=t_cols[:, d, b : b + 1])
+            return scores
+
+        def scores_in_bank(h, picked):
+            bank = psum.tile([P, B, P], F32, name=f"summed{h}")
+            turn(bank, lambda b: t1_wide[:, b, :], True, False)
+            turn(bank, lambda b: picked[:, b, :], False, True)
+            return bank
+
+        def larger(name, a, b, tag, pieces):
+            merged = keep.tile([P, B, P], F32, name=name, tag=tag)
+            for cols in pieces:
+                nc.vector.tensor_tensor(flat(merged)[:, cols], flat(a)[:, cols], flat(b)[:, cols], MAX)
+            return merged
+
+        def turn_back(h, merged):
+            best = psum.tile([P, B, P], F32, name=f"best{h}", tag=f"y{h}")
+            turn(best, lambda b: y_t[h][:, b, :], True, False)
+            turn(best, lambda b: merged[:, b, :], False, True)
+            return flat(best)
+
+        def product(h):
             cols = slice(h * P, (h + 1) * P)
-            nc.tensor.matmul_mx(out=y[h][:], lhsT=w_codes[:, cols].bitcast(FP8X4), lhsT_scale=w_scales[:, cols],
-                                rhs=x_codes[:].bitcast(FP8X4), rhs_scale=x_sc[:], start=True, stop=True)
-        look_up(1, 0)
-        look_up(1, 1)
-        nc.vector.tensor_tensor(res[0][:], y[0][:], m3[0][:], ADD)
+            y_bank = psum.tile([P, B, P], F32, name=f"y_bank{h}", tag=f"y{h}")
+            for b in range(B):
+                states = slice(b * P, (b + 1) * P)
+                nc.tensor.matmul_mx(out=y_bank[:, b, :], lhsT=x_codes[:, states].bitcast(FP8X4), lhsT_scale=x_sc[:, states],
+                                    rhs=w_codes[:, cols].bitcast(FP8X4), rhs_scale=w_scales[:, cols], start=True, stop=True)
+            nc.scalar.copy(y_t[h][:], y_bank[:])
+
+        halves = (slice(0, S // 2), slice(S // 2, S))
+        picked0 = [pick(0, d) for d in range(D)]
+        a00 = scores_by_bias(0, 0, picked0[0])
+        nc.scalar.copy(w_bf[:], w_raw[:].rearrange("p j n -> p n j"))
+        spread(t1_bank, 1, True)
+        nc.scalar.copy(t1_wide[:], t1_bank[:])
+        a02 = scores_by_bias(0, 2, picked0[2])
+        a01 = scores_in_bank(0, picked0[1])
+        nc.vector.quantize_mx(out=w_codes[:].bitcast(FP8X4), scales=w_scales[:], in_=w_bf[:].rearrange("p n j -> p (n j)"))
+        nc.vector.tensor_copy(x_codes[:], words[:].bitcast(U32).indirect(picks[:]))
+        nc.vector.tensor_copy(x_sc[:], scales[:].indirect(picks[:]))
+        product(1)
+        picked10 = pick(1, 0)
+        product(0)
+        sum_bank = psum.tile([P, B, P], F32, name="sum_bank", tag="sum")
+        spread(sum_bank, 2, False)
+        turn(sum_bank, lambda b: y_t[1][:, b, :], False, True)
+        a10 = scores_by_bias(1, 0, picked10)
+        a11 = scores_in_bank(1, pick(1, 1))
+        nc.scalar.copy(y_last[:], flat(sum_bank))
+        two0 = larger("two0", a01, a00, "picked10", halves)
+        three0 = larger("three0", two0, a02, "three0", halves)
+        best0 = turn_back(0, three0)
+        two1 = larger("two1", a11, a10, "two1", [slice(0, S)])
+        best1 = turn_back(1, two1)
+        nc.scalar.copy(res[0][:], best0)
         nc.sync.dma_start(out[0:P, :], res[0][:])
-        nc.vector.tensor_tensor(m2[1][:], cand[1][0][:], cand[1][1][:], MAX)
-        look_up(1, 2)
-        nc.vector.tensor_tensor(m3[1][:], m2[1][:], cand[1][2][:], MAX)
-        nc.vector.tensor_tensor(res[1][:], y[1][:], m3[1][:], ADD)
-        nc.sync.dma_start(out[P : 2 * P, :], res[1][:])
+
+        last = keep.tile([P, S], F32, name="last", tag="scores10")
+        for cols in halves:
+            offsets = pos[2][:, cols.start // 16 : cols.stop // 16]
+            nc.vector.tensor_tensor(last[:, cols], rows[1][:].indirect(offsets), y_last[:, cols], ADD)
+        for cols in halves:
+            nc.vector.tensor_tensor(res[1][:, cols], best1[:, cols], last[:, cols], MAX)
+            nc.sync.dma_start(out[P : 2 * P, cols], res[1][:, cols])

@@ -16,8 +16,10 @@ U16 = mybir.dt.uint16
 U8 = mybir.dt.uint8
 FP8X4 = mybir.dt.float8_e4m3fn_x4
 ADD = mybir.AluOpType.add
+MULT = mybir.AluOpType.mult
 MAX = mybir.AluOpType.max
 IDENTITY = mybir.ActivationFunctionType.Identity
+COPY = mybir.ActivationFunctionType.Copy
 B = S // P
 H = N // P
 QUAD = 32
@@ -32,128 +34,106 @@ def tile_picked_ycrf_vit_p_kernel(tc, x_words, x_scales, w1, alpha, trans, offs,
         pos = [keep.tile([P, S // 16], U16, name=f"pos{d}") for d in range(D)]
         picks = keep.tile([P, S // 16], U16, name="picks")
         rows = [keep.tile([P, U], F32, name=f"alpha{h}") for h in range(H)]
-        words = keep.tile([P, T], I32, name="words")
-        scales = keep.tile([P, T], U8, name="scales", align_bytes=64)
+        words = keep.tile([P, T], I32, name="words", tag="words")
+        scales = keep.tile([P, T], U8, name="scales", tag="scales", align_bytes=64)
         w_raw = keep.tile([P, PACK, N], F32, name="w_raw")
-        w_bf = keep.tile([P, N, PACK], BF16, name="w_bf", align_bytes=64)
+        w_bf = keep.tile([P, N, PACK], BF16, name="w_bf", tag="w_bf", align_bytes=64)
         w_codes = keep.tile([P, N], U32, name="w_codes", align_bytes=64)
         w_scales = keep.tile([P, N], U8, name="w_scales", align_bytes=64)
         x_codes = keep.tile([P, S], U32, name="x_codes", align_bytes=64)
         x_sc = keep.tile([P, S], U8, name="x_sc", align_bytes=64)
         ident = keep.tile([P, P], F32, name="ident")
-        t_rows = keep.tile([P, D, P], F32, name="t_rows")
-        t_cols = keep.tile([P, D, B], F32, name="t_cols")
+        t_rows = keep.tile([P, P], F32, name="t_rows", tag="plain")
+        t_cols = keep.tile([P, 2, B], F32, name="t_cols")
+        t2_wide = keep.tile([P, S], F32, name="t2_wide")
 
-        nc.gpsimd.memset(t_rows[:], 0.0)
-        nc.vector.memset(scales[:].bitcast(I32), 0)
         make_identity(nc, ident[:])
+        nc.gpsimd.memset(scales[:].bitcast(I32), 0)
 
-        nc.sync.dma_start(pos[0][:], pos1)
+        nc.sync.dma_start(t_rows[:], trans[0:2, 0 : P // (2 * B), :].rearrange("d r (b j) -> d (r b) j", b=B))
         nc.sync.dma_start(rows[0][:], alpha[0:P, :])
-        nc.sync.dma_start(pos[1][:], pos2)
-        nc.sync.dma_start(t_rows[0:B, :, :], trans[:, 0, :].rearrange("d (b j) -> b d j", b=B))
+        nc.sync.dma_start(pos[0][:], pos1)
         nc.sync.dma_start(pos[2][:], pos3)
-        nc.sync.dma_start(w_raw[:], w1.rearrange("(p j) n -> p j n", j=PACK))
+        nc.sync.dma_start(t2_wide[:], trans[2])
+        nc.sync.dma_start(pos[1][:], pos2)
+        nc.sync.dma_start(rows[1][:], alpha[P : 2 * P, :])
         nc.sync.dma_start(picks[:], offs)
-        nc.sync.dma_start(words[:], x_words[0].rearrange("p n t -> p (n t)").bitcast(I32))
         for q in range(4):
             nc.sync.dma_start(scales[QUAD * q : QUAD * q + 4, :].bitcast(I32), x_scales[0, 4 * q : 4 * q + 4, :].bitcast(I32))
-        nc.sync.dma_start(rows[1][:], alpha[P : 2 * P, :])
+        nc.sync.dma_start(words[:], x_words[0].rearrange("p n t -> p (n t)").bitcast(I32))
+        nc.sync.dma_start(w_raw[:], w1.rearrange("(p j) n -> p j n", j=PACK))
 
-        def turn(bank, src, first, last):
-            for b in range(B):
-                nc.tensor.matmul(bank[:, b, :], src(b), ident[:], start=(first and b == 0), stop=(last and b == B - 1), is_transpose=True)
+        t_bank = psum.tile([P, 2, P // 2], F32, name="t_bank", tag="y0")
+        nc.tensor.transpose(t_bank[:].rearrange("p d m -> p (d m)"), t_rows[:], ident[:])
+        nc.scalar.copy(t_cols[:], t_bank[:, :, 0:B])
 
-        t_bank = psum.tile([P, B, P], F32, name="t_bank", tag="sum")
-        for d in range(D):
-            nc.tensor.transpose(t_bank[:, d, :], t_rows[:, d, :], ident[:])
-        nc.scalar.copy(t_cols[:], t_bank[:, 0:D, 0:B])
-
-        def spread(bank, d, last):
-            turn(bank, lambda b: t_cols[:, d, b : b + 1].to_broadcast([P, P]), True, last)
+        plain = keep.tile([P, H, 2, B, P], F32, name="plain", tag="plain")
 
         def flat(tile):
             return tile[:].rearrange("p b j -> p (b j)")
 
-        t1_bank = psum.tile([P, B, P], F32, name="t1_bank")
-        t1_wide = keep.tile([P, B, P], F32, name="t1_wide")
-        y_t = [keep.tile([P, B, P], F32, name=f"y_t{h}") for h in range(H)]
-        y_last = keep.tile([P, S], F32, name="y_last")
-        res = [keep.tile([P, S], F32, name=f"res{h}") for h in range(H)]
-
-        def pick(h, d):
-            picked = keep.tile([P, B, P], F32, name=f"picked{h}{d}", tag=f"picked{h}{d}")
-            nc.vector.tensor_copy(flat(picked), rows[h][:].indirect(pos[d][:]))
-            return picked
-
-        def scores_by_bias(h, d, picked):
-            bank = psum.tile([P, B, P], F32, name=f"turned{h}{d}", tag=f"turned{d}")
-            scores = keep.tile([P, B, P], F32, name=f"scores{h}{d}", tag=f"scores{h}{d}")
+        def turned(h, d):
+            picked = plain[:, h, d]
+            nc.scalar.activation(picked.rearrange("p b j -> p (b j)"), rows[h][:].indirect(pos[d][:]), COPY)
+            bank = psum.tile([P, B, P], F32, name=f"turned{h}{d}")
             for b in range(B):
                 nc.tensor.transpose(bank[:, b, :], picked[:, b, :], ident[:])
-            for b in range(B):
-                nc.scalar.activation(scores[:, b, :], bank[:, b, :], IDENTITY, bias=t_cols[:, d, b : b + 1])
-            return scores
-
-        def scores_in_bank(h, picked):
-            bank = psum.tile([P, B, P], F32, name=f"summed{h}")
-            turn(bank, lambda b: t1_wide[:, b, :], True, False)
-            turn(bank, lambda b: picked[:, b, :], False, True)
             return bank
 
-        def larger(name, a, b, tag, pieces):
-            merged = keep.tile([P, B, P], F32, name=name, tag=tag)
-            for cols in pieces:
-                nc.vector.tensor_tensor(flat(merged)[:, cols], flat(a)[:, cols], flat(b)[:, cols], MAX)
-            return merged
-
-        def turn_back(h, merged):
-            best = psum.tile([P, B, P], F32, name=f"best{h}", tag=f"y{h}")
-            turn(best, lambda b: y_t[h][:, b, :], True, False)
-            turn(best, lambda b: merged[:, b, :], False, True)
-            return flat(best)
-
-        def product(h):
-            cols = slice(h * P, (h + 1) * P)
-            y_bank = psum.tile([P, B, P], F32, name=f"y_bank{h}", tag=f"y{h}")
+        def with_weight(h, bank):
+            scores = keep.tile([P, B, P], F32, name=f"scores{h}")
             for b in range(B):
-                states = slice(b * P, (b + 1) * P)
-                nc.tensor.matmul_mx(out=y_bank[:, b, :], lhsT=x_codes[:, states].bitcast(FP8X4), lhsT_scale=x_sc[:, states],
-                                    rhs=w_codes[:, cols].bitcast(FP8X4), rhs_scale=w_scales[:, cols], start=True, stop=True)
-            nc.scalar.copy(y_t[h][:], y_bank[:])
+                nc.scalar.activation(scores[:, b, :], bank[:, b, :], IDENTITY, bias=t_cols[:, 0, b : b + 1])
+            return scores
 
+        def third(h):
+            last = keep.tile([P, S], F32, name=f"last{h}")
+            nc.vector.tensor_tensor(last[:], rows[h][:].indirect(pos[2][:]), t2_wide[:], ADD)
+            return last
+
+        def best_of_two(h, bank, scores, two):
+            for b in range(B):
+                nc.vector.scalar_tensor_tensor(two[:, b, :], bank[:, b, :], t_cols[:, 1, b : b + 1], scores[:, b, :], ADD, MAX)
+            back = psum.tile([P, B, P], F32, name=f"back{h}")
+            for b in range(B):
+                nc.tensor.transpose(back[:, b, :], two[:, b, :], ident[:])
+            return back
+
+        def best_of_three(back, last, three, pieces):
+            for cols in pieces:
+                nc.vector.tensor_tensor(three[:, cols], flat(back)[:, cols], last[:, cols], MAX)
+            return three
+
+        def finish(h, three, pieces):
+            cols = slice(h * P, (h + 1) * P)
+            y_bank = psum.tile([P, S], F32, name=f"y_bank{h}", tag=f"y{h}")
+            nc.tensor.matmul_mx(out=y_bank[:], lhsT=w_codes[:, cols].bitcast(FP8X4), lhsT_scale=w_scales[:, cols],
+                                rhs=x_codes[:].bitcast(FP8X4), rhs_scale=x_sc[:], start=True, stop=True)
+            res = keep.tile([P, S], F32, name=f"res{h}")
+            for part in pieces:
+                nc.vector.tensor_tensor(res[:, part], y_bank[:, part], three[:, part], ADD)
+                nc.sync.dma_start(out[cols, part], res[:, part])
+
+        whole = (slice(0, S),)
         halves = (slice(0, S // 2), slice(S // 2, S))
-        picked0 = [pick(0, d) for d in range(D)]
-        a00 = scores_by_bias(0, 0, picked0[0])
-        nc.scalar.copy(w_bf[:], w_raw[:].rearrange("p j n -> p n j"))
-        spread(t1_bank, 1, True)
-        nc.scalar.copy(t1_wide[:], t1_bank[:])
-        a02 = scores_by_bias(0, 2, picked0[2])
-        a01 = scores_in_bank(0, picked0[1])
-        nc.vector.quantize_mx(out=w_codes[:].bitcast(FP8X4), scales=w_scales[:], in_=w_bf[:].rearrange("p n j -> p (n j)"))
-        nc.vector.tensor_copy(x_codes[:], words[:].bitcast(U32).indirect(picks[:]))
+        bank00 = turned(0, 0)
+        last0 = third(0)
+        bank01 = turned(0, 1)
+        scores0 = with_weight(0, bank00)
+        last1 = third(1)
+        bank10 = turned(1, 0)
         nc.vector.tensor_copy(x_sc[:], scales[:].indirect(picks[:]))
-        product(1)
-        picked10 = pick(1, 0)
-        product(0)
-        sum_bank = psum.tile([P, B, P], F32, name="sum_bank", tag="sum")
-        spread(sum_bank, 2, False)
-        turn(sum_bank, lambda b: y_t[1][:, b, :], False, True)
-        a10 = scores_by_bias(1, 0, picked10)
-        a11 = scores_in_bank(1, pick(1, 1))
-        nc.scalar.copy(y_last[:], flat(sum_bank))
-        two0 = larger("two0", a01, a00, "picked10", halves)
-        three0 = larger("three0", two0, a02, "three0", halves)
-        best0 = turn_back(0, three0)
-        two1 = larger("two1", a11, a10, "two1", [slice(0, S)])
-        best1 = turn_back(1, two1)
-        nc.scalar.copy(res[0][:], best0)
-        nc.sync.dma_start(out[0:P, :], res[0][:])
-
-        last = keep.tile([P, S], F32, name="last", tag="scores10")
-        for cols in halves:
-            offsets = pos[2][:, cols.start // 16 : cols.stop // 16]
-            nc.vector.tensor_tensor(last[:, cols], rows[1][:].indirect(offsets), y_last[:, cols], ADD)
-        for cols in halves:
-            nc.vector.tensor_tensor(res[1][:, cols], best1[:, cols], last[:, cols], MAX)
-            nc.sync.dma_start(out[P : 2 * P, cols], res[1][:, cols])
+        two0 = keep.tile([P, B, P], F32, name="two0", tag="scales", align_bytes=64)
+        back0 = best_of_two(0, bank01, scores0, two0)
+        bank11 = turned(1, 1)
+        scores1 = with_weight(1, bank10)
+        nc.vector.tensor_copy(x_codes[:], words[:].bitcast(U32).indirect(picks[:]))
+        nc.gpsimd.tensor_scalar(w_bf[:], w_raw[:].rearrange("p j n -> p n j"), 1.0, 0.0, MULT, ADD)
+        late = keep.tile([P, 2, B, P], F32, name="late", tag="words")
+        three0 = best_of_three(back0, last0, late[:, 0].rearrange("p b j -> p (b j)"), whole)
+        back1 = best_of_two(1, bank11, scores1, late[:, 1])
+        nc.vector.quantize_mx(out=w_codes[:].bitcast(FP8X4), scales=w_scales[:], in_=w_bf[:].rearrange("p n j -> p (n j)"))
+        three1_tile = keep.tile([P, S], F32, name="three1", tag="w_bf", align_bytes=64)
+        three1 = best_of_three(back1, last1, three1_tile[:], halves)
+        finish(0, three0, whole)
+        finish(1, three1, halves)

@@ -23,38 +23,40 @@ COPY = mybir.ActivationFunctionType.Copy
 B = S // P
 H = N // P
 QUAD = 32
+STEP = 9
+APART = 60
 
 
 def tile_picked_ycrf_vit_p_kernel(tc, x_words, x_scales, w1, alpha, trans, offs, pos1, pos2, pos3, out):
     nc = tc.nc
     with ExitStack() as ctx:
         keep = ctx.enter_context(tc.tile_pool(name="keep", bufs=1))
+        reuse = ctx.enter_context(tc.tile_pool(name="reuse", bufs=1))
         psum = ctx.enter_context(tc.psum_pool(name="psum", bufs=1))
 
         pos = [keep.tile([P, S // 16], U16, name=f"pos{d}") for d in range(D)]
         picks = keep.tile([P, S // 16], U16, name="picks")
         rows = [keep.tile([P, U], F32, name=f"alpha{h}") for h in range(H)]
-        words = keep.tile([P, T], I32, name="words", tag="words")
-        scales = keep.tile([P, T], U8, name="scales", tag="scales", align_bytes=64)
+        words = reuse.tile([P, T], I32, name="words", offset=0)
+        scales = keep.tile([P, T], U8, name="scales", align_bytes=64)
         w_raw = keep.tile([P, PACK, N], F32, name="w_raw")
-        w_bf = keep.tile([P, N, PACK], BF16, name="w_bf", tag="w_bf", align_bytes=64)
-        w_codes = keep.tile([P, N], U32, name="w_codes", align_bytes=64)
+        w_bf = keep.tile([P, N, PACK], BF16, name="w_bf", align_bytes=64)
         w_scales = keep.tile([P, N], U8, name="w_scales", align_bytes=64)
-        x_codes = keep.tile([P, S], U32, name="x_codes", align_bytes=64)
-        x_sc = keep.tile([P, S], U8, name="x_sc", align_bytes=64)
         ident = keep.tile([P, P], F32, name="ident")
-        t_rows = keep.tile([P, P], F32, name="t_rows", tag="plain")
-        t_cols = keep.tile([P, 2, B], F32, name="t_cols")
+        t_rows = keep.tile([P, P], F32, name="t_rows")
+        ident_bf = keep.tile([P, P], BF16, name="ident_bf", tag="plain")
+        t_cols = keep.tile([P, D, B], F32, name="t_cols")
         t2_wide = keep.tile([P, S], F32, name="t2_wide")
 
-        make_identity(nc, ident[:])
+        make_identity(nc, ident_bf[:])
         nc.gpsimd.memset(scales[:].bitcast(I32), 0)
+        nc.scalar.copy(ident[:], ident_bf[:])
 
-        nc.sync.dma_start(t_rows[:], trans[0:2, 0 : P // (2 * B), :].rearrange("d r (b j) -> d (r b) j", b=B))
         nc.sync.dma_start(rows[0][:], alpha[0:P, :])
         nc.sync.dma_start(pos[0][:], pos1)
         nc.sync.dma_start(pos[2][:], pos3)
         nc.sync.dma_start(t2_wide[:], trans[2])
+        nc.sync.dma_start(t_rows[:], trans.rearrange("d r (b j) -> (d r b) j", b=B)[0 : P * STEP : STEP, :])
         nc.sync.dma_start(pos[1][:], pos2)
         nc.sync.dma_start(rows[1][:], alpha[P : 2 * P, :])
         nc.sync.dma_start(picks[:], offs)
@@ -63,77 +65,89 @@ def tile_picked_ycrf_vit_p_kernel(tc, x_words, x_scales, w1, alpha, trans, offs,
         nc.sync.dma_start(words[:], x_words[0].rearrange("p n t -> p (n t)").bitcast(I32))
         nc.sync.dma_start(w_raw[:], w1.rearrange("(p j) n -> p j n", j=PACK))
 
-        t_bank = psum.tile([P, 2, P // 2], F32, name="t_bank", tag="y0")
-        nc.tensor.transpose(t_bank[:].rearrange("p d m -> p (d m)"), t_rows[:], ident[:])
+        t_bank = psum.tile([P, D, APART], F32, name="t_bank", tag="y0")
+        nc.tensor.transpose(t_bank[:].rearrange("p d m -> p (d m)")[:, 0:P], t_rows[:], ident[:])
         nc.scalar.copy(t_cols[:], t_bank[:, :, 0:B])
-
-        plain = keep.tile([P, H, 2, B, P], F32, name="plain", tag="plain")
 
         def flat(tile):
             return tile[:].rearrange("p b j -> p (b j)")
 
-        def turned(h, d):
-            picked = plain[:, h, d]
-            nc.scalar.activation(picked.rearrange("p b j -> p (b j)"), rows[h][:].indirect(pos[d][:]), COPY)
-            bank = psum.tile([P, B, P], F32, name=f"turned{h}{d}")
+        def turn(bank, src, first, last):
             for b in range(B):
-                nc.tensor.transpose(bank[:, b, :], picked[:, b, :], ident[:])
-            return bank
+                nc.tensor.matmul(bank[:, b, :], src[:, b, :], ident[:], start=(first and b == 0), stop=(last and b == B - 1), is_transpose=True)
+
+        def turned(h, d, gather, picked, bank_tags):
+            gather(picked.rearrange("p b j -> p (b j)"), rows[h][:].indirect(pos[d][:]))
+            per = B // len(bank_tags)
+            banks = [psum.tile([P, per, P], F32, name=f"turned{h}{d}{tag}", tag=tag) for tag in bank_tags]
+            blocks = [banks[b // per][:, b % per, :] for b in range(B)]
+            for b in range(B):
+                nc.tensor.transpose(blocks[b], picked[:, b, :], ident[:])
+            return blocks
+
+        def on_scalar(dst, src):
+            nc.scalar.activation(dst, src, COPY)
 
         def with_weight(h, bank):
-            scores = keep.tile([P, B, P], F32, name=f"scores{h}")
+            scores = [keep.tile([P, 2, P], F32, name=f"scores{h}{i}", tag=f"scores{h}{i}", align_bytes=64) for i in range(2)]
+            blocks = [scores[b // 2][:, b % 2, :] for b in range(B)]
             for b in range(B):
-                nc.scalar.activation(scores[:, b, :], bank[:, b, :], IDENTITY, bias=t_cols[:, 0, b : b + 1])
-            return scores
+                nc.scalar.activation(blocks[b], bank[b], IDENTITY, bias=t_cols[:, 0, b : b + 1])
+            return blocks
 
-        def third(h):
-            last = keep.tile([P, S], F32, name=f"last{h}")
-            nc.vector.tensor_tensor(last[:], rows[h][:].indirect(pos[2][:]), t2_wide[:], ADD)
-            return last
-
-        def best_of_two(h, bank, scores, two):
+        def larger(dst, bank, d, scores):
             for b in range(B):
-                nc.vector.scalar_tensor_tensor(two[:, b, :], bank[:, b, :], t_cols[:, 1, b : b + 1], scores[:, b, :], ADD, MAX)
-            back = psum.tile([P, B, P], F32, name=f"back{h}")
-            for b in range(B):
-                nc.tensor.transpose(back[:, b, :], two[:, b, :], ident[:])
-            return back
+                nc.vector.scalar_tensor_tensor(dst[:, b, :], bank[b], t_cols[:, d, b : b + 1], scores[b], ADD, MAX)
 
-        def best_of_three(back, last, three, pieces):
-            for cols in pieces:
-                nc.vector.tensor_tensor(three[:, cols], flat(back)[:, cols], last[:, cols], MAX)
-            return three
-
-        def finish(h, three, pieces):
-            cols = slice(h * P, (h + 1) * P)
-            y_bank = psum.tile([P, S], F32, name=f"y_bank{h}", tag=f"y{h}")
-            nc.tensor.matmul_mx(out=y_bank[:], lhsT=w_codes[:, cols].bitcast(FP8X4), lhsT_scale=w_scales[:, cols],
-                                rhs=x_codes[:].bitcast(FP8X4), rhs_scale=x_sc[:], start=True, stop=True)
-            res = keep.tile([P, S], F32, name=f"res{h}")
-            for part in pieces:
-                nc.vector.tensor_tensor(res[:, part], y_bank[:, part], three[:, part], ADD)
-                nc.sync.dma_start(out[cols, part], res[:, part])
-
-        whole = (slice(0, S),)
         halves = (slice(0, S // 2), slice(S // 2, S))
-        bank00 = turned(0, 0)
-        last0 = third(0)
-        bank01 = turned(0, 1)
+
+        def third(h, dst, cols):
+            nc.vector.tensor_tensor(dst, rows[h][:].indirect(pos[2][:, cols.start // 16 : cols.stop // 16]), t2_wide[:, cols], ADD)
+
+        def product(h, tag):
+            cols = slice(h * P, (h + 1) * P)
+            bank = psum.tile([P, S], F32, name=f"y{h}", tag=tag)
+            nc.tensor.matmul_mx(out=bank[:], lhsT=w_codes[:, cols].bitcast(FP8X4), lhsT_scale=w_scales[:, cols],
+                                rhs=x_codes[:].bitcast(FP8X4), rhs_scale=x_sc[:], start=True, stop=True)
+            return bank
+
+        whole = slice(0, S)
+        last = [keep.tile([P, S], F32, name=f"last{h}") for h in range(H)]
+        res = [keep.tile([P, S], F32, name=f"res{h}") for h in range(H)]
+        plain0 = keep.tile([P, 2, B, P], F32, name="plain0", tag="plain")
+        bank00 = turned(0, 0, on_scalar, plain0[:, 0], ["b0"])
+        third(0, last[0][:], whole)
+        bank01 = turned(0, 1, on_scalar, plain0[:, 1], ["b1"])
         scores0 = with_weight(0, bank00)
-        last1 = third(1)
-        bank10 = turned(1, 0)
+        third(1, last[1][:], whole)
+        plain1 = keep.tile([P, 2, B, P], F32, name="plain1", tag="plain")
+        two0 = keep.tile([P, B, P], F32, name="two0")
+        larger(two0, bank01, 1, scores0)
+        back0 = psum.tile([P, B, P], F32, name="back0")
+        turn(back0, two0, True, True)
+        bank10 = turned(1, 0, on_scalar, plain1[:, 0], ["b0"])
+        x_sc = keep.tile([P, S], U8, name="x_sc", tag="scores00", align_bytes=64)
+        x_codes = keep.tile([P, S], U32, name="x_codes", tag="scores01", align_bytes=64)
         nc.vector.tensor_copy(x_sc[:], scales[:].indirect(picks[:]))
-        two0 = keep.tile([P, B, P], F32, name="two0", tag="scales", align_bytes=64)
-        back0 = best_of_two(0, bank01, scores0, two0)
-        bank11 = turned(1, 1)
-        scores1 = with_weight(1, bank10)
         nc.vector.tensor_copy(x_codes[:], words[:].bitcast(U32).indirect(picks[:]))
+        bank11 = turned(1, 1, on_scalar, plain1[:, 1], ["b4"])
+        scores1 = with_weight(1, bank10)
         nc.gpsimd.tensor_scalar(w_bf[:], w_raw[:].rearrange("p j n -> p n j"), 1.0, 0.0, MULT, ADD)
-        late = keep.tile([P, 2, B, P], F32, name="late", tag="words")
-        three0 = best_of_three(back0, last0, late[:, 0].rearrange("p b j -> p (b j)"), whole)
-        back1 = best_of_two(1, bank11, scores1, late[:, 1])
+        three0 = reuse.tile([P, S], F32, name="three0", offset=0)
+        nc.vector.tensor_tensor(three0[:], flat(back0), last[0][:], MAX)
+        w_codes = reuse.tile([P, N], U32, name="w_codes", offset=2048, align_bytes=64)
         nc.vector.quantize_mx(out=w_codes[:].bitcast(FP8X4), scales=w_scales[:], in_=w_bf[:].rearrange("p n j -> p (n j)"))
-        three1_tile = keep.tile([P, S], F32, name="three1", tag="w_bf", align_bytes=64)
-        three1 = best_of_three(back1, last1, three1_tile[:], halves)
-        finish(0, three0, whole)
-        finish(1, three1, halves)
+        two1 = reuse.tile([P, B, P], F32, name="two1", offset=4096)
+        larger(two1, bank11, 1, scores1)
+        y0 = product(0, "y0")
+        y1 = product(1, "b1")
+        back1 = psum.tile([P, B, P], F32, name="back1")
+        turn(back1, two1, True, True)
+        nc.vector.tensor_tensor(res[0][:], y0[:], three0[:], ADD)
+        nc.sync.dma_start(out[0:P, :], res[0][:])
+        three1 = keep.tile([P, S], F32, name="three1")
+        for cols in halves:
+            nc.vector.tensor_tensor(three1[:, cols], flat(back1)[:, cols], last[1][:, cols], MAX)
+        for cols in halves:
+            nc.vector.tensor_tensor(res[1][:, cols], y1[:, cols], three1[:, cols], ADD)
+            nc.sync.dma_start(out[P:N, cols], res[1][:, cols])

@@ -31,19 +31,20 @@ def tile_picked_ycrf_vit_p_kernel(tc, x_words, x_scales, w1, alpha, trans, offs,
     nc = tc.nc
     with ExitStack() as ctx:
         keep = ctx.enter_context(tc.tile_pool(name="keep", bufs=1))
-        reuse = ctx.enter_context(tc.tile_pool(name="reuse", bufs=1))
         psum = ctx.enter_context(tc.psum_pool(name="psum", bufs=1))
 
         pos = [keep.tile([P, S // 16], U16, name=f"pos{d}") for d in range(D)]
         picks = keep.tile([P, S // 16], U16, name="picks")
         rows = [keep.tile([P, U], F32, name=f"alpha{h}") for h in range(H)]
-        words = reuse.tile([P, T], I32, name="words", offset=0)
-        scales = keep.tile([P, T], U8, name="scales", align_bytes=64)
+        words = keep.tile([P, T], I32, name="words", tag="words")
+        scales = keep.tile([P, T], U8, name="scales", tag="scales", align_bytes=64)
         w_raw = keep.tile([P, PACK, N], F32, name="w_raw")
-        w_bf = keep.tile([P, N, PACK], BF16, name="w_bf", align_bytes=64)
-        w_scales = keep.tile([P, N], U8, name="w_scales", align_bytes=64)
+        w_bf = [keep.tile([P, P, PACK], BF16, name=f"w_bf{h}", tag=f"w_bf{h}", align_bytes=64) for h in range(H)]
+        w_codes = [keep.tile([P, P], U32, name=f"w_codes{h}", align_bytes=64) for h in range(H)]
+        w_scales = [keep.tile([P, P], U8, name=f"w_scales{h}", align_bytes=64) for h in range(H)]
+        x_sc = keep.tile([P, S], U8, name="x_sc", align_bytes=64)
         ident = keep.tile([P, P], F32, name="ident")
-        t_rows = keep.tile([P, P], F32, name="t_rows")
+        t_rows = keep.tile([P, P], F32, name="t_rows", tag="t_rows")
         ident_bf = keep.tile([P, P], BF16, name="ident_bf", tag="plain")
         t_cols = keep.tile([P, D, B], F32, name="t_cols")
         t2_wide = keep.tile([P, S], F32, name="t2_wide")
@@ -69,85 +70,93 @@ def tile_picked_ycrf_vit_p_kernel(tc, x_words, x_scales, w1, alpha, trans, offs,
         nc.tensor.transpose(t_bank[:].rearrange("p d m -> p (d m)")[:, 0:P], t_rows[:], ident[:])
         nc.scalar.copy(t_cols[:], t_bank[:, :, 0:B])
 
-        def flat(tile):
-            return tile[:].rearrange("p b j -> p (b j)")
+        halves = (slice(0, S // 2), slice(S // 2, S))
+        whole = slice(0, S)
 
-        def turn(bank, src, first, last):
-            for b in range(B):
-                nc.tensor.matmul(bank[:, b, :], src[:, b, :], ident[:], start=(first and b == 0), stop=(last and b == B - 1), is_transpose=True)
+        def offsets(lst, cols):
+            return lst[:, cols.start // 16 : cols.stop // 16]
 
-        def turned(h, d, gather, picked, bank_tags):
-            gather(picked.rearrange("p b j -> p (b j)"), rows[h][:].indirect(pos[d][:]))
-            per = B // len(bank_tags)
-            banks = [psum.tile([P, per, P], F32, name=f"turned{h}{d}{tag}", tag=tag) for tag in bank_tags]
-            blocks = [banks[b // per][:, b % per, :] for b in range(B)]
-            for b in range(B):
-                nc.tensor.transpose(blocks[b], picked[:, b, :], ident[:])
-            return blocks
+        def turn(src, name, tag):
+            bank = psum.tile([P, src.shape[1]], F32, name=name, tag=tag)
+            for b in range(src.shape[1] // P):
+                nc.tensor.transpose(bank[:, b * P : (b + 1) * P], src[:, b * P : (b + 1) * P], ident[:])
+            return bank
 
-        def on_scalar(dst, src):
-            nc.scalar.activation(dst, src, COPY)
+        def pick(dst, h, d, cols):
+            nc.scalar.activation(dst, rows[h][:].indirect(offsets(pos[d], cols)), COPY)
 
         def with_weight(h, bank):
-            scores = [keep.tile([P, 2, P], F32, name=f"scores{h}{i}", tag=f"scores{h}{i}", align_bytes=64) for i in range(2)]
-            blocks = [scores[b // 2][:, b % 2, :] for b in range(B)]
+            scores = [keep.tile([P, S // 2], F32, name=f"scores{h}{i}", tag=f"scores{h}{i}", align_bytes=64) for i in range(2)]
             for b in range(B):
-                nc.scalar.activation(blocks[b], bank[b], IDENTITY, bias=t_cols[:, 0, b : b + 1])
-            return blocks
+                block = slice(b % 2 * P, (b % 2 + 1) * P)
+                nc.scalar.activation(scores[b // 2][:, block], bank[:, b * P : (b + 1) * P], IDENTITY, bias=t_cols[:, 0, b : b + 1])
+            return scores
 
-        def larger(dst, bank, d, scores):
-            for b in range(B):
-                nc.vector.scalar_tensor_tensor(dst[:, b, :], bank[b], t_cols[:, d, b : b + 1], scores[b], ADD, MAX)
-
-        halves = (slice(0, S // 2), slice(S // 2, S))
+        def larger(dst, bank, scores, i):
+            for b in range(2):
+                block = slice(b * P, (b + 1) * P)
+                nc.vector.scalar_tensor_tensor(dst[:, block], bank[:, block], t_cols[:, 1, 2 * i + b : 2 * i + b + 1], scores[:, block], ADD, MAX)
 
         def third(h, dst, cols):
-            nc.vector.tensor_tensor(dst, rows[h][:].indirect(pos[2][:, cols.start // 16 : cols.stop // 16]), t2_wide[:, cols], ADD)
+            nc.vector.tensor_tensor(dst, rows[h][:].indirect(offsets(pos[2], cols)), t2_wide[:, cols], ADD)
+
+        def quantise(h):
+            nc.vector.quantize_mx(out=w_codes[h][:].bitcast(FP8X4), scales=w_scales[h][:], in_=w_bf[h][:].rearrange("p n j -> p (n j)"))
 
         def product(h, tag):
-            cols = slice(h * P, (h + 1) * P)
             bank = psum.tile([P, S], F32, name=f"y{h}", tag=tag)
-            nc.tensor.matmul_mx(out=bank[:], lhsT=w_codes[:, cols].bitcast(FP8X4), lhsT_scale=w_scales[:, cols],
+            nc.tensor.matmul_mx(out=bank[:], lhsT=w_codes[h][:].bitcast(FP8X4), lhsT_scale=w_scales[h][:],
                                 rhs=x_codes[:].bitcast(FP8X4), rhs_scale=x_sc[:], start=True, stop=True)
             return bank
 
-        whole = slice(0, S)
-        last = [keep.tile([P, S], F32, name=f"last{h}") for h in range(H)]
         res = [keep.tile([P, S], F32, name=f"res{h}") for h in range(H)]
-        plain0 = keep.tile([P, 2, B, P], F32, name="plain0", tag="plain")
-        bank00 = turned(0, 0, on_scalar, plain0[:, 0], ["b0"])
-        third(0, last[0][:], whole)
-        bank01 = turned(0, 1, on_scalar, plain0[:, 1], ["b1"])
+        plain0 = keep.tile([P, 2, S], F32, name="plain0", tag="plain")
+        pick(plain0[:, 0], 0, 0, whole)
+        bank00 = turn(plain0[:, 0], "turned00", "b0")
+        last0 = keep.tile([P, S], F32, name="last0")
+        third(0, last0[:], whole)
+        pick(plain0[:, 1], 0, 1, whole)
+        bank01 = turn(plain0[:, 1], "turned01", "b1")
         scores0 = with_weight(0, bank00)
-        third(1, last[1][:], whole)
-        plain1 = keep.tile([P, 2, B, P], F32, name="plain1", tag="plain")
-        two0 = keep.tile([P, B, P], F32, name="two0")
-        larger(two0, bank01, 1, scores0)
-        back0 = psum.tile([P, B, P], F32, name="back0")
-        turn(back0, two0, True, True)
-        bank10 = turned(1, 0, on_scalar, plain1[:, 0], ["b0"])
-        x_sc = keep.tile([P, S], U8, name="x_sc", tag="scores00", align_bytes=64)
-        x_codes = keep.tile([P, S], U32, name="x_codes", tag="scores01", align_bytes=64)
+        last1 = [keep.tile([P, S // 2], F32, name=f"last1{i}") for i in range(2)]
+        third(1, last1[0][:], halves[0])
+        picked12 = keep.tile([P, S // 2], F32, name="picked12", tag="t_rows")
+        pick(picked12[:], 1, 2, halves[1])
+        nc.gpsimd.tensor_tensor(last1[1][:], picked12[:], t2_wide[:, halves[1]], ADD)
         nc.vector.tensor_copy(x_sc[:], scales[:].indirect(picks[:]))
+        two0 = keep.tile([P, S], F32, name="two0", tag="scales", align_bytes=64)
+        for i, cols in enumerate(halves):
+            larger(two0[:, cols], bank01[:, cols], scores0[i], i)
+        back0 = turn(two0[:], "back0", "b2")
+
+        x_codes = keep.tile([P, S], U32, name="x_codes", tag="scores01", align_bytes=64)
         nc.vector.tensor_copy(x_codes[:], words[:].bitcast(U32).indirect(picks[:]))
-        bank11 = turned(1, 1, on_scalar, plain1[:, 1], ["b4"])
+        three0 = keep.tile([P, S], F32, name="three0", tag="words")
+        nc.vector.tensor_tensor(three0[:], back0[:], last0[:], MAX)
+
+        plain1 = keep.tile([P, 2, S], F32, name="plain1", tag="plain")
+        pick(plain1[:, 0], 1, 0, whole)
+        bank10 = turn(plain1[:, 0], "turned10", "b0")
+        bank11 = []
+        for cols, tag in zip(halves, ("b1", "b3")):
+            pick(plain1[:, 1, cols], 1, 1, cols)
+            bank11.append(turn(plain1[:, 1, cols], f"turned11{tag}", tag))
         scores1 = with_weight(1, bank10)
-        nc.gpsimd.tensor_scalar(w_bf[:], w_raw[:].rearrange("p j n -> p n j"), 1.0, 0.0, MULT, ADD)
-        three0 = reuse.tile([P, S], F32, name="three0", offset=0)
-        nc.vector.tensor_tensor(three0[:], flat(back0), last[0][:], MAX)
-        w_codes = reuse.tile([P, N], U32, name="w_codes", offset=2048, align_bytes=64)
-        nc.vector.quantize_mx(out=w_codes[:].bitcast(FP8X4), scales=w_scales[:], in_=w_bf[:].rearrange("p n j -> p (n j)"))
-        two1 = reuse.tile([P, B, P], F32, name="two1", offset=4096)
-        larger(two1, bank11, 1, scores1)
+        for h in range(H):
+            nc.gpsimd.tensor_scalar(w_bf[h][:], w_raw[:, :, h * P : (h + 1) * P].rearrange("p j n -> p n j"), 1.0, 0.0, MULT, ADD)
+            quantise(h)
         y0 = product(0, "y0")
-        y1 = product(1, "b1")
-        back1 = psum.tile([P, B, P], F32, name="back1")
-        turn(back1, two1, True, True)
+        two1 = keep.tile([P, S], F32, name="two1", tag="w_bf0", align_bytes=64)
+        back1 = []
+        for i, cols in enumerate(halves):
+            larger(two1[:, cols], bank11[i], scores1[i], i)
+            back1.append(turn(two1[:, cols], f"back1{i}", f"b{4 + i}"))
+        y1 = product(1, "b3")
         nc.vector.tensor_tensor(res[0][:], y0[:], three0[:], ADD)
         nc.sync.dma_start(out[0:P, :], res[0][:])
         three1 = keep.tile([P, S], F32, name="three1")
-        for cols in halves:
-            nc.vector.tensor_tensor(three1[:, cols], flat(back1)[:, cols], last[1][:, cols], MAX)
+        for i, cols in enumerate(halves):
+            nc.vector.tensor_tensor(three1[:, cols], back1[i][:], last1[i][:], MAX)
         for cols in halves:
             nc.vector.tensor_tensor(res[1][:, cols], y1[:, cols], three1[:, cols], ADD)
             nc.sync.dma_start(out[P:N, cols], res[1][:, cols])

@@ -31,26 +31,27 @@ def tile_picked_ycrf_vit_p_kernel(tc, x_words, x_scales, w1, alpha, trans, offs,
     nc = tc.nc
     with ExitStack() as ctx:
         keep = ctx.enter_context(tc.tile_pool(name="keep", bufs=1))
+        reuse = ctx.enter_context(tc.tile_pool(name="reuse", bufs=1))
         psum = ctx.enter_context(tc.psum_pool(name="psum", bufs=1))
 
         pos = [keep.tile([P, S // 16], U16, name=f"pos{d}") for d in range(D)]
         picks = keep.tile([P, S // 16], U16, name="picks")
         rows = [keep.tile([P, U], F32, name=f"alpha{h}") for h in range(H)]
-        words = keep.tile([P, T], I32, name="words", tag="words")
+        words = reuse.tile([P, T], I32, name="words", offset=0)
         scales = keep.tile([P, T], U8, name="scales", tag="scales", align_bytes=64)
         w_raw = keep.tile([P, PACK, N], F32, name="w_raw")
-        w_bf = [keep.tile([P, P, PACK], BF16, name=f"w_bf{h}", tag=f"w_bf{h}", align_bytes=64) for h in range(H)]
-        w_codes = [keep.tile([P, P], U32, name=f"w_codes{h}", align_bytes=64) for h in range(H)]
         w_scales = [keep.tile([P, P], U8, name=f"w_scales{h}", align_bytes=64) for h in range(H)]
         x_sc = keep.tile([P, S], U8, name="x_sc", align_bytes=64)
+        x_rows = keep.tile([P, S], U8, name="x_rows", align_bytes=64)
         ident = keep.tile([P, P], F32, name="ident")
-        t_rows = keep.tile([P, P], F32, name="t_rows", tag="t_rows")
-        ident_bf = keep.tile([P, P], BF16, name="ident_bf", tag="plain")
+        t_rows = keep.tile([P, P], F32, name="t_rows", tag="second")
+        ident_bf = keep.tile([P, P], BF16, name="ident_bf", tag="first")
         t_cols = keep.tile([P, D, B], F32, name="t_cols")
         t2_wide = keep.tile([P, S], F32, name="t2_wide")
 
         make_identity(nc, ident_bf[:])
         nc.gpsimd.memset(scales[:].bitcast(I32), 0)
+        nc.gpsimd.memset(x_sc[:].bitcast(I32), 0)
         nc.scalar.copy(ident[:], ident_bf[:])
 
         nc.sync.dma_start(rows[0][:], alpha[0:P, :])
@@ -61,8 +62,7 @@ def tile_picked_ycrf_vit_p_kernel(tc, x_words, x_scales, w1, alpha, trans, offs,
         nc.sync.dma_start(pos[1][:], pos2)
         nc.sync.dma_start(rows[1][:], alpha[P : 2 * P, :])
         nc.sync.dma_start(picks[:], offs)
-        for q in range(4):
-            nc.sync.dma_start(scales[QUAD * q : QUAD * q + 4, :].bitcast(I32), x_scales[0, 4 * q : 4 * q + 4, :].bitcast(I32))
+        nc.sync.dma_start(scales[0:16, :].bitcast(I32), x_scales[0].bitcast(I32))
         nc.sync.dma_start(words[:], x_words[0].rearrange("p n t -> p (n t)").bitcast(I32))
         nc.sync.dma_start(w_raw[:], w1.rearrange("(p j) n -> p j n", j=PACK))
 
@@ -86,72 +86,77 @@ def tile_picked_ycrf_vit_p_kernel(tc, x_words, x_scales, w1, alpha, trans, offs,
             nc.scalar.activation(dst, rows[h][:].indirect(offsets(pos[d], cols)), COPY)
 
         def with_weight(h, bank):
-            scores = [keep.tile([P, S // 2], F32, name=f"scores{h}{i}", tag=f"scores{h}{i}", align_bytes=64) for i in range(2)]
+            scores = [keep.tile([P, P], F32, name=f"scores{h}{b}", tag=f"scores{h}{b}", align_bytes=64) for b in range(B)]
             for b in range(B):
-                block = slice(b % 2 * P, (b % 2 + 1) * P)
-                nc.scalar.activation(scores[b // 2][:, block], bank[:, b * P : (b + 1) * P], IDENTITY, bias=t_cols[:, 0, b : b + 1])
+                nc.scalar.activation(scores[b][:], bank[:, b * P : (b + 1) * P], IDENTITY, bias=t_cols[:, 0, b : b + 1])
             return scores
 
         def larger(dst, bank, scores, i):
             for b in range(2):
                 block = slice(b * P, (b + 1) * P)
-                nc.vector.scalar_tensor_tensor(dst[:, block], bank[:, block], t_cols[:, 1, 2 * i + b : 2 * i + b + 1], scores[:, block], ADD, MAX)
+                nc.vector.scalar_tensor_tensor(dst[:, block], bank[:, block], t_cols[:, 1, 2 * i + b : 2 * i + b + 1], scores[2 * i + b][:], ADD, MAX)
 
         def third(h, dst, cols):
             nc.vector.tensor_tensor(dst, rows[h][:].indirect(offsets(pos[2], cols)), t2_wide[:, cols], ADD)
 
-        def quantise(h):
-            nc.vector.quantize_mx(out=w_codes[h][:].bitcast(FP8X4), scales=w_scales[h][:], in_=w_bf[h][:].rearrange("p n j -> p (n j)"))
-
-        def product(h, tag):
+        def product(h, codes, tag):
             bank = psum.tile([P, S], F32, name=f"y{h}", tag=tag)
-            nc.tensor.matmul_mx(out=bank[:], lhsT=w_codes[h][:].bitcast(FP8X4), lhsT_scale=w_scales[h][:],
+            nc.tensor.matmul_mx(out=bank[:], lhsT=codes[:].bitcast(FP8X4), lhsT_scale=w_scales[h][:],
                                 rhs=x_codes[:].bitcast(FP8X4), rhs_scale=x_sc[:], start=True, stop=True)
             return bank
 
-        res = [keep.tile([P, S], F32, name=f"res{h}") for h in range(H)]
-        plain0 = keep.tile([P, 2, S], F32, name="plain0", tag="plain")
-        pick(plain0[:, 0], 0, 0, whole)
-        bank00 = turn(plain0[:, 0], "turned00", "b0")
-        last0 = keep.tile([P, S], F32, name="last0")
+        picked00 = keep.tile([P, S], F32, name="picked00", tag="first")
+        pick(picked00[:], 0, 0, whole)
+        bank00 = turn(picked00[:], "turned00", "b0")
+        last0 = keep.tile([P, S], F32, name="last0", tag="last0")
         third(0, last0[:], whole)
-        pick(plain0[:, 1], 0, 1, whole)
-        bank01 = turn(plain0[:, 1], "turned01", "b1")
+        picked01 = keep.tile([P, S], F32, name="picked01", tag="second")
+        pick(picked01[:], 0, 1, whole)
+        bank01 = turn(picked01[:], "turned01", "b1")
         scores0 = with_weight(0, bank00)
-        last1 = [keep.tile([P, S // 2], F32, name=f"last1{i}") for i in range(2)]
+        last1 = [keep.tile([P, S // 2], F32, name="last1a")]
         third(1, last1[0][:], halves[0])
-        picked12 = keep.tile([P, S // 2], F32, name="picked12", tag="t_rows")
+        picked12 = keep.tile([P, S // 2], F32, name="picked12", tag="first")
         pick(picked12[:], 1, 2, halves[1])
+        nc.vector.tensor_copy(x_rows[:], scales[:].indirect(picks[:]))
+        for q in range(4):
+            nc.sync.dma_start(x_sc[QUAD * q : QUAD * q + 4, :].bitcast(I32), x_rows[4 * q : 4 * q + 4, :].bitcast(I32))
+        last1.append(keep.tile([P, S // 2], F32, name="last1b", tag="scales", align_bytes=64))
         nc.gpsimd.tensor_tensor(last1[1][:], picked12[:], t2_wide[:, halves[1]], ADD)
-        nc.vector.tensor_copy(x_sc[:], scales[:].indirect(picks[:]))
-        two0 = keep.tile([P, S], F32, name="two0", tag="scales", align_bytes=64)
+        two0 = keep.tile([P, S], F32, name="two0")
         for i, cols in enumerate(halves):
-            larger(two0[:, cols], bank01[:, cols], scores0[i], i)
+            larger(two0[:, cols], bank01[:, cols], scores0, i)
         back0 = turn(two0[:], "back0", "b2")
 
-        x_codes = keep.tile([P, S], U32, name="x_codes", tag="scores01", align_bytes=64)
+        x_codes = keep.tile([P, S], U32, name="x_codes", tag="scores02", align_bytes=64)
         nc.vector.tensor_copy(x_codes[:], words[:].bitcast(U32).indirect(picks[:]))
-        three0 = keep.tile([P, S], F32, name="three0", tag="words")
+        three0 = keep.tile([P, S], F32, name="three0")
         nc.vector.tensor_tensor(three0[:], back0[:], last0[:], MAX)
 
-        plain1 = keep.tile([P, 2, S], F32, name="plain1", tag="plain")
-        pick(plain1[:, 0], 1, 0, whole)
-        bank10 = turn(plain1[:, 0], "turned10", "b0")
+        picked10 = keep.tile([P, S], F32, name="picked10", tag="second")
+        picked11 = keep.tile([P, S], F32, name="picked11", tag="first")
+        pick(picked10[:], 1, 0, whole)
+        bank10 = turn(picked10[:], "turned10", "b0")
         bank11 = []
         for cols, tag in zip(halves, ("b1", "b3")):
-            pick(plain1[:, 1, cols], 1, 1, cols)
-            bank11.append(turn(plain1[:, 1, cols], f"turned11{tag}", tag))
+            pick(picked11[:, cols], 1, 1, cols)
+            bank11.append(turn(picked11[:, cols], f"turned11{tag}", tag))
         scores1 = with_weight(1, bank10)
-        for h in range(H):
-            nc.gpsimd.tensor_scalar(w_bf[h][:], w_raw[:, :, h * P : (h + 1) * P].rearrange("p j n -> p n j"), 1.0, 0.0, MULT, ADD)
-            quantise(h)
-        y0 = product(0, "y0")
-        two1 = keep.tile([P, S], F32, name="two1", tag="w_bf0", align_bytes=64)
+        def weights(h, tag):
+            w_bf = reuse.tile([P, P, PACK], BF16, name=f"w_bf{h}", offset=0, align_bytes=64)
+            nc.gpsimd.tensor_scalar(w_bf[:], w_raw[:, :, h * P : (h + 1) * P].rearrange("p j n -> p n j"), 1.0, 0.0, MULT, ADD)
+            codes = keep.tile([P, P], U32, name=f"w_codes{h}", tag=tag, align_bytes=64)
+            nc.vector.quantize_mx(out=codes[:].bitcast(FP8X4), scales=w_scales[h][:], in_=w_bf[:].rearrange("p n j -> p (n j)"))
+            return codes
+
+        y0 = product(0, weights(0, "w_codes0"), "y0")
+        two1 = keep.tile([P, S], F32, name="two1", tag="last0")
         back1 = []
         for i, cols in enumerate(halves):
-            larger(two1[:, cols], bank11[i], scores1[i], i)
+            larger(two1[:, cols], bank11[i], scores1, i)
             back1.append(turn(two1[:, cols], f"back1{i}", f"b{4 + i}"))
-        y1 = product(1, "b3")
+        y1 = product(1, weights(1, "scores12"), "b3")
+        res = [keep.tile([P, S], F32, name="res0", tag="scores13", align_bytes=64), keep.tile([P, S], F32, name="res1")]
         nc.vector.tensor_tensor(res[0][:], y0[:], three0[:], ADD)
         nc.sync.dma_start(out[0:P, :], res[0][:])
         three1 = keep.tile([P, S], F32, name="three1")

@@ -40,11 +40,12 @@ def tile_picked_ycrf_vit_p_kernel(tc, x_words, x_scales, w1, alpha, trans, offs,
         words = reuse.tile([P, T], I32, name="words", offset=0)
         scales = keep.tile([P, T], U8, name="scales", tag="scales", align_bytes=64)
         w_raw = keep.tile([P, PACK, N], F32, name="w_raw")
-        w_scales = [keep.tile([P, P], U8, name=f"w_scales{h}", align_bytes=64) for h in range(H)]
+        w_codes = keep.tile([P, N], U32, name="w_codes", align_bytes=64)
+        w_scales = keep.tile([P, N], U8, name="w_scales", align_bytes=64)
         x_sc = keep.tile([P, S], U8, name="x_sc", align_bytes=64)
         x_rows = keep.tile([P, S], U8, name="x_rows", align_bytes=64)
         ident = keep.tile([P, P], F32, name="ident")
-        t_rows = keep.tile([P, P], F32, name="t_rows", tag="second")
+        t_rows = reuse.tile([P, P], F32, name="t_rows", offset=9216)
         ident_bf = keep.tile([P, P], BF16, name="ident_bf", tag="first")
         t_cols = keep.tile([P, D, B], F32, name="t_cols")
         t2_wide = keep.tile([P, S], F32, name="t2_wide")
@@ -60,11 +61,11 @@ def tile_picked_ycrf_vit_p_kernel(tc, x_words, x_scales, w1, alpha, trans, offs,
         nc.sync.dma_start(t2_wide[:], trans[2])
         nc.sync.dma_start(t_rows[:], trans.rearrange("d r (b j) -> (d r b) j", b=B)[0 : P * STEP : STEP, :])
         nc.sync.dma_start(pos[1][:], pos2)
-        nc.sync.dma_start(rows[1][:], alpha[P : 2 * P, :])
         nc.sync.dma_start(picks[:], offs)
-        nc.sync.dma_start(scales[0:16, :].bitcast(I32), x_scales[0].bitcast(I32))
-        nc.sync.dma_start(words[:], x_words[0].rearrange("p n t -> p (n t)").bitcast(I32))
         nc.sync.dma_start(w_raw[:], w1.rearrange("(p j) n -> p j n", j=PACK))
+        nc.sync.dma_start(scales[0:16, :].bitcast(I32), x_scales[0].bitcast(I32))
+        nc.sync.dma_start(rows[1][:], alpha[P : 2 * P, :])
+        nc.sync.dma_start(words[:], x_words[0].rearrange("p n t -> p (n t)").bitcast(I32))
 
         t_bank = psum.tile([P, D, APART], F32, name="t_bank", tag="y0")
         nc.tensor.transpose(t_bank[:].rearrange("p d m -> p (d m)")[:, 0:P], t_rows[:], ident[:])
@@ -96,45 +97,46 @@ def tile_picked_ycrf_vit_p_kernel(tc, x_words, x_scales, w1, alpha, trans, offs,
                 block = slice(b * P, (b + 1) * P)
                 nc.vector.scalar_tensor_tensor(dst[:, block], bank[:, block], t_cols[:, 1, 2 * i + b : 2 * i + b + 1], scores[2 * i + b][:], ADD, MAX)
 
-        def third(h, dst, cols):
-            nc.vector.tensor_tensor(dst, rows[h][:].indirect(offsets(pos[2], cols)), t2_wide[:, cols], ADD)
-
-        def product(h, codes, tag):
+        def product(h, tag):
+            cols = slice(h * P, (h + 1) * P)
             bank = psum.tile([P, S], F32, name=f"y{h}", tag=tag)
-            nc.tensor.matmul_mx(out=bank[:], lhsT=codes[:].bitcast(FP8X4), lhsT_scale=w_scales[h][:],
+            nc.tensor.matmul_mx(out=bank[:], lhsT=w_codes[:, cols].bitcast(FP8X4), lhsT_scale=w_scales[:, cols],
                                 rhs=x_codes[:].bitcast(FP8X4), rhs_scale=x_sc[:], start=True, stop=True)
             return bank
 
         picked00 = keep.tile([P, S], F32, name="picked00", tag="first")
         pick(picked00[:], 0, 0, whole)
         bank00 = turn(picked00[:], "turned00", "b0")
-        last0 = keep.tile([P, S], F32, name="last0", tag="last0")
-        third(0, last0[:], whole)
-        picked01 = keep.tile([P, S], F32, name="picked01", tag="second")
+        last0 = keep.tile([P, S], F32, name="last0")
+        nc.vector.tensor_tensor(last0[:], rows[0][:].indirect(pos[2][:]), t2_wide[:], ADD)
+        picked01 = reuse.tile([P, S], F32, name="picked01", offset=9216)
         pick(picked01[:], 0, 1, whole)
         bank01 = turn(picked01[:], "turned01", "b1")
         scores0 = with_weight(0, bank00)
-        last1 = [keep.tile([P, S // 2], F32, name="last1a")]
-        third(1, last1[0][:], halves[0])
         picked12 = keep.tile([P, S // 2], F32, name="picked12", tag="first")
         pick(picked12[:], 1, 2, halves[1])
+        w_bf = keep.tile([P, N, PACK], BF16, name="w_bf", align_bytes=64)
+        nc.vector.tensor_copy(w_bf[:], w_raw[:].rearrange("p j n -> p n j"))
         nc.vector.tensor_copy(x_rows[:], scales[:].indirect(picks[:]))
         for q in range(4):
             nc.sync.dma_start(x_sc[QUAD * q : QUAD * q + 4, :].bitcast(I32), x_rows[4 * q : 4 * q + 4, :].bitcast(I32))
-        last1.append(keep.tile([P, S // 2], F32, name="last1b", tag="scales", align_bytes=64))
-        nc.gpsimd.tensor_tensor(last1[1][:], picked12[:], t2_wide[:, halves[1]], ADD)
-        two0 = keep.tile([P, S], F32, name="two0")
+        nc.vector.quantize_mx(out=w_codes[:].bitcast(FP8X4), scales=w_scales[:], in_=w_bf[:].rearrange("p n j -> p (n j)"))
+        two0 = keep.tile([P, S], F32, name="two0", tag="scales", align_bytes=64)
         for i, cols in enumerate(halves):
             larger(two0[:, cols], bank01[:, cols], scores0, i)
         back0 = turn(two0[:], "back0", "b2")
 
+        last1 = [keep.tile([P, S // 2], F32, name="last1a", tag="scores00", align_bytes=64)]
+        nc.vector.tensor_tensor(last1[0][:], rows[1][:].indirect(offsets(pos[2], halves[0])), t2_wide[:, halves[0]], ADD)
         x_codes = keep.tile([P, S], U32, name="x_codes", tag="scores02", align_bytes=64)
         nc.vector.tensor_copy(x_codes[:], words[:].bitcast(U32).indirect(picks[:]))
-        three0 = keep.tile([P, S], F32, name="three0")
+        three0 = reuse.tile([P, S], F32, name="three0", offset=0)
         nc.vector.tensor_tensor(three0[:], back0[:], last0[:], MAX)
+        last1.append(reuse.tile([P, S // 2], F32, name="last1b", offset=2048))
+        nc.gpsimd.tensor_tensor(last1[1][:], picked12[:], t2_wide[:, halves[1]], ADD)
 
-        picked10 = keep.tile([P, S], F32, name="picked10", tag="second")
-        picked11 = keep.tile([P, S], F32, name="picked11", tag="first")
+        picked10 = reuse.tile([P, S], F32, name="picked10", offset=8192)
+        picked11 = reuse.tile([P, S], F32, name="picked11", offset=10240)
         pick(picked10[:], 1, 0, whole)
         bank10 = turn(picked10[:], "turned10", "b0")
         bank11 = []
@@ -142,21 +144,15 @@ def tile_picked_ycrf_vit_p_kernel(tc, x_words, x_scales, w1, alpha, trans, offs,
             pick(picked11[:, cols], 1, 1, cols)
             bank11.append(turn(picked11[:, cols], f"turned11{tag}", tag))
         scores1 = with_weight(1, bank10)
-        def weights(h, tag):
-            w_bf = reuse.tile([P, P, PACK], BF16, name=f"w_bf{h}", offset=0, align_bytes=64)
-            nc.gpsimd.tensor_scalar(w_bf[:], w_raw[:, :, h * P : (h + 1) * P].rearrange("p j n -> p n j"), 1.0, 0.0, MULT, ADD)
-            codes = keep.tile([P, P], U32, name=f"w_codes{h}", tag=tag, align_bytes=64)
-            nc.vector.quantize_mx(out=codes[:].bitcast(FP8X4), scales=w_scales[h][:], in_=w_bf[:].rearrange("p n j -> p (n j)"))
-            return codes
 
-        y0 = product(0, weights(0, "w_codes0"), "y0")
-        two1 = keep.tile([P, S], F32, name="two1", tag="last0")
+        y0 = product(0, "y0")
+        y1 = product(1, "b6")
+        two1 = reuse.tile([P, S], F32, name="two1", offset=4096)
         back1 = []
         for i, cols in enumerate(halves):
             larger(two1[:, cols], bank11[i], scores1, i)
             back1.append(turn(two1[:, cols], f"back1{i}", f"b{4 + i}"))
-        y1 = product(1, weights(1, "scores12"), "b3")
-        res = [keep.tile([P, S], F32, name="res0", tag="scores13", align_bytes=64), keep.tile([P, S], F32, name="res1")]
+        res = [keep.tile([P, S], F32, name="res0", tag="scores12", align_bytes=64), keep.tile([P, S], F32, name="res1")]
         nc.vector.tensor_tensor(res[0][:], y0[:], three0[:], ADD)
         nc.sync.dma_start(out[0:P, :], res[0][:])
         three1 = keep.tile([P, S], F32, name="three1")

@@ -23,8 +23,6 @@ COPY = mybir.ActivationFunctionType.Copy
 B = S // P
 H = N // P
 QUAD = 32
-STEP = 9
-APART = 60
 
 
 def tile_picked_ycrf_vit_p_kernel(tc, x_words, x_scales, w1, alpha, trans, offs, pos1, pos2, pos3, out):
@@ -47,9 +45,10 @@ def tile_picked_ycrf_vit_p_kernel(tc, x_words, x_scales, w1, alpha, trans, offs,
         ident = keep.tile([P, P], F32, name="ident")
         t_rows = reuse.tile([P, P], F32, name="t_rows", offset=9216)
         ident_bf = keep.tile([P, P], BF16, name="ident_bf", tag="first")
-        t_cols = keep.tile([P, D, B], F32, name="t_cols")
+        t_cols = keep.tile([P, 2, B], F32, name="t_cols")
         t2_wide = keep.tile([P, S], F32, name="t2_wide")
 
+        nc.gpsimd.memset(t_rows[:], 0.0)
         make_identity(nc, ident_bf[:])
         nc.gpsimd.memset(scales[:].bitcast(I32), 0)
         nc.gpsimd.memset(x_sc[:].bitcast(I32), 0)
@@ -59,7 +58,7 @@ def tile_picked_ycrf_vit_p_kernel(tc, x_words, x_scales, w1, alpha, trans, offs,
         nc.sync.dma_start(pos[0][:], pos1)
         nc.sync.dma_start(pos[2][:], pos3)
         nc.sync.dma_start(t2_wide[:], trans[2])
-        nc.sync.dma_start(t_rows[:], trans.rearrange("d r (b j) -> (d r b) j", b=B)[0 : P * STEP : STEP, :])
+        nc.sync.dma_start(t_rows[0 : 2 * B, :], trans[0:2, 0, :].rearrange("d (b j) -> d b j", b=B))
         nc.sync.dma_start(pos[1][:], pos2)
         nc.sync.dma_start(picks[:], offs)
         nc.sync.dma_start(w_raw[:], w1.rearrange("(p j) n -> p j n", j=PACK))
@@ -67,9 +66,9 @@ def tile_picked_ycrf_vit_p_kernel(tc, x_words, x_scales, w1, alpha, trans, offs,
         nc.sync.dma_start(rows[1][:], alpha[P : 2 * P, :])
         nc.sync.dma_start(words[:], x_words[0].rearrange("p n t -> p (n t)").bitcast(I32))
 
-        t_bank = psum.tile([P, D, APART], F32, name="t_bank", tag="y0")
-        nc.tensor.transpose(t_bank[:].rearrange("p d m -> p (d m)")[:, 0:P], t_rows[:], ident[:])
-        nc.scalar.copy(t_cols[:], t_bank[:, :, 0:B])
+        t_bank = psum.tile([P, P], F32, name="t_bank", tag="y0")
+        nc.tensor.transpose(t_bank[:], t_rows[:], ident[:])
+        nc.scalar.copy(t_cols[:].rearrange("p d b -> p (d b)"), t_bank[:, 0 : 2 * B])
 
         halves = (slice(0, S // 2), slice(S // 2, S))
         whole = slice(0, S)
@@ -116,7 +115,7 @@ def tile_picked_ycrf_vit_p_kernel(tc, x_words, x_scales, w1, alpha, trans, offs,
         picked12 = keep.tile([P, S // 2], F32, name="picked12", tag="first")
         pick(picked12[:], 1, 2, halves[1])
         w_bf = keep.tile([P, N, PACK], BF16, name="w_bf", align_bytes=64)
-        nc.vector.tensor_copy(w_bf[:], w_raw[:].rearrange("p j n -> p n j"))
+        nc.vector.tensor_copy(w_bf[:].rearrange("p (c i) j -> p c j i", i=PACK), w_raw[:].rearrange("p j (c i) -> p c j i", i=PACK))
         nc.vector.tensor_copy(x_rows[:], scales[:].indirect(picks[:]))
         for q in range(4):
             nc.sync.dma_start(x_sc[QUAD * q : QUAD * q + 4, :].bitcast(I32), x_rows[4 * q : 4 * q + 4, :].bitcast(I32))
@@ -130,7 +129,7 @@ def tile_picked_ycrf_vit_p_kernel(tc, x_words, x_scales, w1, alpha, trans, offs,
         nc.vector.tensor_tensor(last1[0][:], rows[1][:].indirect(offsets(pos[2], halves[0])), t2_wide[:, halves[0]], ADD)
         x_codes = keep.tile([P, S], U32, name="x_codes", tag="scores02", align_bytes=64)
         nc.vector.tensor_copy(x_codes[:], words[:].bitcast(U32).indirect(picks[:]))
-        three0 = reuse.tile([P, S], F32, name="three0", offset=0)
+        three0 = keep.tile([P, S], F32, name="three0")
         nc.vector.tensor_tensor(three0[:], back0[:], last0[:], MAX)
         last1.append(reuse.tile([P, S // 2], F32, name="last1b", offset=2048))
         nc.gpsimd.tensor_tensor(last1[1][:], picked12[:], t2_wide[:, halves[1]], ADD)

@@ -23,6 +23,10 @@ COPY = mybir.ActivationFunctionType.Copy
 B = S // P
 H = N // P
 QUAD = 32
+SCALE_ROWS = K // 32
+SCALES_AT = P - SCALE_ROWS
+T_ROWS = 2 * B
+T_AT = P - T_ROWS
 
 
 def tile_picked_ycrf_vit_p_kernel(tc, x_words, x_scales, w1, alpha, trans, offs, pos1, pos2, pos3, out):
@@ -35,40 +39,40 @@ def tile_picked_ycrf_vit_p_kernel(tc, x_words, x_scales, w1, alpha, trans, offs,
         pos = [keep.tile([P, S // 16], U16, name=f"pos{d}") for d in range(D)]
         picks = keep.tile([P, S // 16], U16, name="picks")
         rows = [keep.tile([P, U], F32, name=f"alpha{h}") for h in range(H)]
-        words = reuse.tile([P, T], I32, name="words", offset=0)
-        scales = keep.tile([P, T], U8, name="scales", tag="scales", align_bytes=64)
+        words = keep.tile([P, T], I32, name="words", tag="words", align_bytes=64)
+        scales = keep.tile([P, T], U8, name="scales")
         w_raw = keep.tile([P, PACK, N], F32, name="w_raw")
-        w_codes = keep.tile([P, N], U32, name="w_codes", align_bytes=64)
-        w_scales = keep.tile([P, N], U8, name="w_scales", align_bytes=64)
+        w_codes = [keep.tile([P, P], U32, name=f"w_codes{h}", align_bytes=64) for h in range(H)]
+        w_scales = [keep.tile([P, P], U8, name=f"w_scales{h}", align_bytes=64) for h in range(H)]
         x_sc = keep.tile([P, S], U8, name="x_sc", align_bytes=64)
         x_rows = keep.tile([P, S], U8, name="x_rows", align_bytes=64)
         ident = keep.tile([P, P], F32, name="ident")
-        t_rows = reuse.tile([P, P], F32, name="t_rows", offset=9216)
-        ident_bf = keep.tile([P, P], BF16, name="ident_bf", tag="first")
+        t_rows = reuse.tile([P, P], F32, name="t_rows", offset=8192)
+        ident_bf = reuse.tile([P, P], BF16, name="ident_bf", offset=2048)
         t_cols = keep.tile([P, 2, B], F32, name="t_cols")
         t2_wide = keep.tile([P, S], F32, name="t2_wide")
 
-        nc.gpsimd.memset(t_rows[:], 0.0)
         make_identity(nc, ident_bf[:])
-        nc.gpsimd.memset(scales[:].bitcast(I32), 0)
+        nc.gpsimd.memset(t_rows[0:T_AT, :], 0.0)
         nc.gpsimd.memset(x_sc[:].bitcast(I32), 0)
+        nc.vector.memset(scales[0:SCALES_AT, :].bitcast(I32), 0)
         nc.scalar.copy(ident[:], ident_bf[:])
 
+        nc.sync.dma_start(picks[:], offs)
+        nc.scalar.dma_start(t_rows[T_AT:P, :], trans[0:2, 0, :].rearrange("d (b j) -> d b j", b=B))
+        nc.sync.dma_start(scales[SCALES_AT:P, :].bitcast(I32), x_scales[0].bitcast(I32))
         nc.sync.dma_start(rows[0][:], alpha[0:P, :])
         nc.sync.dma_start(pos[0][:], pos1)
+        nc.sync.dma_start(pos[1][:], pos2)
         nc.sync.dma_start(pos[2][:], pos3)
         nc.sync.dma_start(t2_wide[:], trans[2])
-        nc.sync.dma_start(t_rows[0 : 2 * B, :], trans[0:2, 0, :].rearrange("d (b j) -> d b j", b=B))
-        nc.sync.dma_start(pos[1][:], pos2)
-        nc.sync.dma_start(picks[:], offs)
-        nc.sync.dma_start(w_raw[:], w1.rearrange("(p j) n -> p j n", j=PACK))
-        nc.sync.dma_start(scales[0:16, :].bitcast(I32), x_scales[0].bitcast(I32))
         nc.sync.dma_start(rows[1][:], alpha[P : 2 * P, :])
         nc.sync.dma_start(words[:], x_words[0].rearrange("p n t -> p (n t)").bitcast(I32))
+        nc.sync.dma_start(w_raw[:], w1.rearrange("(p j) n -> p j n", j=PACK))
 
         t_bank = psum.tile([P, P], F32, name="t_bank", tag="y0")
         nc.tensor.transpose(t_bank[:], t_rows[:], ident[:])
-        nc.scalar.copy(t_cols[:].rearrange("p d b -> p (d b)"), t_bank[:, 0 : 2 * B])
+        nc.scalar.copy(t_cols[:].rearrange("p d b -> p (d b)"), t_bank[:, T_AT:P])
 
         halves = (slice(0, S // 2), slice(S // 2, S))
         whole = slice(0, S)
@@ -97,66 +101,73 @@ def tile_picked_ycrf_vit_p_kernel(tc, x_words, x_scales, w1, alpha, trans, offs,
                 nc.vector.scalar_tensor_tensor(dst[:, block], bank[:, block], t_cols[:, 1, 2 * i + b : 2 * i + b + 1], scores[2 * i + b][:], ADD, MAX)
 
         def product(h, tag):
-            cols = slice(h * P, (h + 1) * P)
             bank = psum.tile([P, S], F32, name=f"y{h}", tag=tag)
-            nc.tensor.matmul_mx(out=bank[:], lhsT=w_codes[:, cols].bitcast(FP8X4), lhsT_scale=w_scales[:, cols],
+            nc.tensor.matmul_mx(out=bank[:], lhsT=w_codes[h][:].bitcast(FP8X4), lhsT_scale=w_scales[h][:],
                                 rhs=x_codes[:].bitcast(FP8X4), rhs_scale=x_sc[:], start=True, stop=True)
             return bank
 
-        picked00 = keep.tile([P, S], F32, name="picked00", tag="first")
-        pick(picked00[:], 0, 0, whole)
-        bank00 = turn(picked00[:], "turned00", "b0")
-        last0 = keep.tile([P, S], F32, name="last0")
-        nc.vector.tensor_tensor(last0[:], rows[0][:].indirect(pos[2][:]), t2_wide[:], ADD)
-        picked01 = reuse.tile([P, S], F32, name="picked01", offset=9216)
-        pick(picked01[:], 0, 1, whole)
-        bank01 = turn(picked01[:], "turned01", "b1")
-        scores0 = with_weight(0, bank00)
-        picked12 = keep.tile([P, S // 2], F32, name="picked12", tag="first")
-        pick(picked12[:], 1, 2, halves[1])
-        w_bf = keep.tile([P, N, PACK], BF16, name="w_bf", align_bytes=64)
-        nc.vector.tensor_copy(w_bf[:].rearrange("p (c i) j -> p c j i", i=PACK), w_raw[:].rearrange("p j (c i) -> p c j i", i=PACK))
+        def rounding(w_bf, h):
+            return w_bf[:].rearrange("p (c i) j -> p c j i", i=PACK), w_raw[:, :, h * P : (h + 1) * P].rearrange("p j (c i) -> p c j i", i=PACK)
+
+        def quantise(h, w_bf):
+            nc.vector.quantize_mx(out=w_codes[h][:].bitcast(FP8X4), scales=w_scales[h][:], in_=w_bf[:].rearrange("p n j -> p (n j)"))
+
         nc.vector.tensor_copy(x_rows[:], scales[:].indirect(picks[:]))
         for q in range(4):
-            nc.sync.dma_start(x_sc[QUAD * q : QUAD * q + 4, :].bitcast(I32), x_rows[4 * q : 4 * q + 4, :].bitcast(I32))
-        nc.vector.quantize_mx(out=w_codes[:].bitcast(FP8X4), scales=w_scales[:], in_=w_bf[:].rearrange("p n j -> p (n j)"))
-        two0 = keep.tile([P, S], F32, name="two0", tag="scales", align_bytes=64)
-        for i, cols in enumerate(halves):
-            larger(two0[:, cols], bank01[:, cols], scores0, i)
-        back0 = turn(two0[:], "back0", "b2")
+            nc.sync.dma_start(x_sc[QUAD * q : QUAD * q + 4, :].bitcast(I32), x_rows[SCALES_AT + 4 * q : SCALES_AT + 4 * q + 4, :].bitcast(I32))
 
-        last1 = [keep.tile([P, S // 2], F32, name="last1a", tag="scores00", align_bytes=64)]
-        nc.vector.tensor_tensor(last1[0][:], rows[1][:].indirect(offsets(pos[2], halves[0])), t2_wide[:, halves[0]], ADD)
-        x_codes = keep.tile([P, S], U32, name="x_codes", tag="scores02", align_bytes=64)
-        nc.vector.tensor_copy(x_codes[:], words[:].bitcast(U32).indirect(picks[:]))
-        three0 = keep.tile([P, S], F32, name="three0")
-        nc.vector.tensor_tensor(three0[:], back0[:], last0[:], MAX)
-        last1.append(reuse.tile([P, S // 2], F32, name="last1b", offset=2048))
+        picked00 = reuse.tile([P, S], F32, name="picked00", offset=128)
+        pick(picked00[:], 0, 0, whole)
+        picked01 = [keep.tile([P, S // 2], F32, name="picked01a"), reuse.tile([P, S // 2], F32, name="picked01b", offset=7424)]
+        nc.vector.tensor_copy(picked01[0][:], rows[0][:].indirect(offsets(pos[1], halves[0])))
+        bank01 = [turn(picked01[0][:], "turned01a", "b1")]
+        bank00 = turn(picked00[:], "turned00", "b0")
+        last0 = keep.tile([P, S], F32, name="last0")
+        last1 = [keep.tile([P, S // 2], F32, name=f"last1{i}") for i in range(2)]
+        nc.vector.tensor_tensor(last0[:], rows[0][:].indirect(pos[2][:]), t2_wide[:], ADD)
+        pick(picked01[1][:], 0, 1, halves[1])
+        bank01.append(turn(picked01[1][:], "turned01b", "b3"))
+        picked12 = reuse.tile([P, S // 2], F32, name="picked12", offset=2176)
+        pick(picked12[:], 1, 2, halves[1])
         nc.gpsimd.tensor_tensor(last1[1][:], picked12[:], t2_wide[:, halves[1]], ADD)
+        scores0 = with_weight(0, bank00)
+        nc.vector.tensor_tensor(last1[0][:], rows[1][:].indirect(offsets(pos[2], halves[0])), t2_wide[:, halves[0]], ADD)
+        two0 = keep.tile([P, S], F32, name="two0")
+        for i, cols in enumerate(halves):
+            larger(two0[:, cols], bank01[i], scores0, i)
 
-        picked10 = reuse.tile([P, S], F32, name="picked10", offset=8192)
-        picked11 = reuse.tile([P, S], F32, name="picked11", offset=10240)
+        back0 = turn(two0[:], "back0", "b2")
+        picked10 = reuse.tile([P, S], F32, name="picked10", offset=128)
         pick(picked10[:], 1, 0, whole)
         bank10 = turn(picked10[:], "turned10", "b0")
+        picked11 = [reuse.tile([P, S // 2], F32, name="picked11a", offset=7488), reuse.tile([P, S // 2], F32, name="picked11b", offset=6464)]
         bank11 = []
-        for cols, tag in zip(halves, ("b1", "b3")):
-            pick(picked11[:, cols], 1, 1, cols)
-            bank11.append(turn(picked11[:, cols], f"turned11{tag}", tag))
+        for i, tag in enumerate(("b1", "b3")):
+            pick(picked11[i][:], 1, 1, halves[i])
+            bank11.append(turn(picked11[i][:], f"turned11{tag}", tag))
         scores1 = with_weight(1, bank10)
 
-        y0 = product(0, "y0")
-        y1 = product(1, "b6")
-        two1 = reuse.tile([P, S], F32, name="two1", offset=4096)
-        back1 = []
-        for i, cols in enumerate(halves):
-            larger(two1[:, cols], bank11[i], scores1, i)
-            back1.append(turn(two1[:, cols], f"back1{i}", f"b{4 + i}"))
+        x_codes = keep.tile([P, S], U32, name="x_codes", tag="scores02", align_bytes=64)
+        nc.vector.tensor_copy(x_codes[:], words[:].bitcast(U32).indirect(picks[:]))
+        w_bf = [keep.tile([P, P, PACK], BF16, name="w_bf0", tag="words", align_bytes=64), reuse.tile([P, P, PACK], BF16, name="w_bf1", offset=0, align_bytes=64)]
+        nc.gpsimd.tensor_scalar(w_bf[0][:], w_raw[:, :, 0:P].rearrange("p j n -> p n j"), 1.0, 0.0, MULT, ADD)
+        nc.scalar.copy(*rounding(w_bf[1], 1))
+        two1 = keep.tile([P, S], F32, name="two1")
+        three = [keep.tile([P, S], F32, name=f"three{h}") for h in range(H)]
         res = [keep.tile([P, S], F32, name="res0", tag="scores12", align_bytes=64), keep.tile([P, S], F32, name="res1")]
-        nc.vector.tensor_tensor(res[0][:], y0[:], three0[:], ADD)
+        nc.vector.tensor_tensor(three[0][:], back0[:], last0[:], MAX)
+        larger(two1[:, halves[0]], bank11[0], scores1, 0)
+        back1 = [turn(two1[:, halves[0]], "back10", "b4")]
+        quantise(0, w_bf[0])
+        y0 = product(0, "y0")
+        larger(two1[:, halves[1]], bank11[1], scores1, 1)
+        back1.append(turn(two1[:, halves[1]], "back11", "b5"))
+        quantise(1, w_bf[1])
+        y1 = product(1, "b6")
+        nc.vector.tensor_tensor(res[0][:], y0[:], three[0][:], ADD)
         nc.sync.dma_start(out[0:P, :], res[0][:])
-        three1 = keep.tile([P, S], F32, name="three1")
         for i, cols in enumerate(halves):
-            nc.vector.tensor_tensor(three1[:, cols], back1[i][:], last1[i][:], MAX)
+            nc.vector.tensor_tensor(three[1][:, cols], back1[i][:], last1[i][:], MAX)
         for cols in halves:
-            nc.vector.tensor_tensor(res[1][:, cols], y1[:, cols], three1[:, cols], ADD)
+            nc.vector.tensor_tensor(res[1][:, cols], y1[:, cols], three[1][:, cols], ADD)
             nc.sync.dma_start(out[P:N, cols], res[1][:, cols])

@@ -39,17 +39,15 @@ def tile_picked_ycrf_vit_p_kernel(tc, x_words, x_scales, w1, alpha, trans, offs,
         pos = [keep.tile([P, S // 16], U16, name=f"pos{d}") for d in range(D)]
         picks = keep.tile([P, S // 16], U16, name="picks")
         rows = [keep.tile([P, U], F32, name=f"alpha{h}") for h in range(H)]
-        words = keep.tile([P, T], I32, name="words", tag="words", align_bytes=64)
+        words = reuse.tile([P, T], I32, name="words", offset=16384)
         scales = keep.tile([P, T], U8, name="scales")
-        w_raw = keep.tile([P, PACK, N], F32, name="w_raw")
-        w_codes = [keep.tile([P, P], U32, name=f"w_codes{h}", align_bytes=64) for h in range(H)]
+        w_raw = keep.tile([P, PACK, N], F32, name="w_raw", tag="w_raw")
         w_scales = [keep.tile([P, P], U8, name=f"w_scales{h}", align_bytes=64) for h in range(H)]
         x_sc = keep.tile([P, S], U8, name="x_sc", align_bytes=64)
         x_rows = keep.tile([P, S], U8, name="x_rows", align_bytes=64)
         ident = keep.tile([P, P], F32, name="ident")
-        t_rows = reuse.tile([P, P], F32, name="t_rows", offset=8192)
-        ident_bf = reuse.tile([P, P], BF16, name="ident_bf", offset=2048)
-        t_cols = keep.tile([P, 2, B], F32, name="t_cols")
+        t_rows = keep.tile([P, P], F32, name="t_rows")
+        ident_bf = reuse.tile([P, P], BF16, name="ident_bf", offset=4096 - 128)
         t2_wide = keep.tile([P, S], F32, name="t2_wide")
 
         make_identity(nc, ident_bf[:])
@@ -59,20 +57,16 @@ def tile_picked_ycrf_vit_p_kernel(tc, x_words, x_scales, w1, alpha, trans, offs,
         nc.scalar.copy(ident[:], ident_bf[:])
 
         nc.sync.dma_start(picks[:], offs)
-        nc.scalar.dma_start(t_rows[T_AT:P, :], trans[0:2, 0, :].rearrange("d (b j) -> d b j", b=B))
         nc.sync.dma_start(scales[SCALES_AT:P, :].bitcast(I32), x_scales[0].bitcast(I32))
         nc.sync.dma_start(rows[0][:], alpha[0:P, :])
         nc.sync.dma_start(pos[0][:], pos1)
         nc.sync.dma_start(pos[1][:], pos2)
         nc.sync.dma_start(pos[2][:], pos3)
+        nc.sync.dma_start(t_rows[T_AT:P, :], trans[0:2, 0, :].rearrange("d (b j) -> d b j", b=B))
         nc.sync.dma_start(t2_wide[:], trans[2])
         nc.sync.dma_start(rows[1][:], alpha[P : 2 * P, :])
-        nc.sync.dma_start(words[:], x_words[0].rearrange("p n t -> p (n t)").bitcast(I32))
         nc.sync.dma_start(w_raw[:], w1.rearrange("(p j) n -> p j n", j=PACK))
-
-        t_bank = psum.tile([P, P], F32, name="t_bank", tag="y0")
-        nc.tensor.transpose(t_bank[:], t_rows[:], ident[:])
-        nc.scalar.copy(t_cols[:].rearrange("p d b -> p (d b)"), t_bank[:, T_AT:P])
+        nc.sync.dma_start(words[:], x_words[0].rearrange("p n t -> p (n t)").bitcast(I32))
 
         halves = (slice(0, S // 2), slice(S // 2, S))
         whole = slice(0, S)
@@ -112,56 +106,67 @@ def tile_picked_ycrf_vit_p_kernel(tc, x_words, x_scales, w1, alpha, trans, offs,
         def quantise(h, w_bf):
             nc.vector.quantize_mx(out=w_codes[h][:].bitcast(FP8X4), scales=w_scales[h][:], in_=w_bf[:].rearrange("p n j -> p (n j)"))
 
+        def turn_into(bank, src, cols):
+            for b in range(src.shape[1] // P):
+                nc.tensor.transpose(bank[:, cols.start + b * P : cols.start + (b + 1) * P], src[:, b * P : (b + 1) * P], ident[:])
+
         nc.vector.tensor_copy(x_rows[:], scales[:].indirect(picks[:]))
         for q in range(4):
             nc.sync.dma_start(x_sc[QUAD * q : QUAD * q + 4, :].bitcast(I32), x_rows[SCALES_AT + 4 * q : SCALES_AT + 4 * q + 4, :].bitcast(I32))
 
-        picked00 = reuse.tile([P, S], F32, name="picked00", offset=128)
-        pick(picked00[:], 0, 0, whole)
-        picked01 = [keep.tile([P, S // 2], F32, name="picked01a"), reuse.tile([P, S // 2], F32, name="picked01b", offset=7424)]
-        nc.vector.tensor_copy(picked01[0][:], rows[0][:].indirect(offsets(pos[1], halves[0])))
-        bank01 = [turn(picked01[0][:], "turned01a", "b1")]
-        bank00 = turn(picked00[:], "turned00", "b0")
+        picked00 = [keep.tile([P, S // 2], F32, name="picked00a", tag="picked00a"), reuse.tile([P, S // 2], F32, name="picked00b", offset=3072)]
+        bank00 = psum.tile([P, S], F32, name="turned00", tag="b0")
+        nc.vector.tensor_copy(picked00[0][:], rows[0][:].indirect(offsets(pos[0], halves[0])))
+        pick(picked00[1][:], 0, 0, halves[1])
+        t_bank = psum.tile([P, P], F32, name="t_bank", tag="y0")
+        nc.tensor.transpose(t_bank[:], t_rows[:], ident[:])
+        for i, cols in enumerate(halves):
+            turn_into(bank00, picked00[i][:], cols)
+        picked01 = reuse.tile([P, S], F32, name="picked01", offset=4096)
+        bank01 = []
+        for cols, tag in zip(halves, ("b1", "b3")):
+            pick(picked01[:, cols], 0, 1, cols)
+            bank01.append(turn(picked01[:, cols], f"turned01{tag}", tag))
+        t_cols = keep.tile([P, 2, B], F32, name="t_cols", tag="picked00a")
+        nc.scalar.copy(t_cols[:].rearrange("p d b -> p (d b)"), t_bank[:, T_AT:P])
         last0 = keep.tile([P, S], F32, name="last0")
-        last1 = [keep.tile([P, S // 2], F32, name=f"last1{i}") for i in range(2)]
         nc.vector.tensor_tensor(last0[:], rows[0][:].indirect(pos[2][:]), t2_wide[:], ADD)
-        pick(picked01[1][:], 0, 1, halves[1])
-        bank01.append(turn(picked01[1][:], "turned01b", "b3"))
-        picked12 = reuse.tile([P, S // 2], F32, name="picked12", offset=2176)
-        pick(picked12[:], 1, 2, halves[1])
-        nc.gpsimd.tensor_tensor(last1[1][:], picked12[:], t2_wide[:, halves[1]], ADD)
         scores0 = with_weight(0, bank00)
+        last1 = [keep.tile([P, S // 2], F32, name="last1a")]
         nc.vector.tensor_tensor(last1[0][:], rows[1][:].indirect(offsets(pos[2], halves[0])), t2_wide[:, halves[0]], ADD)
-        two0 = keep.tile([P, S], F32, name="two0")
+        two0 = reuse.tile([P, S], F32, name="two0", offset=9216)
         for i, cols in enumerate(halves):
             larger(two0[:, cols], bank01[i], scores0, i)
-
         back0 = turn(two0[:], "back0", "b2")
-        picked10 = reuse.tile([P, S], F32, name="picked10", offset=128)
+        last1.append(keep.tile([P, S // 2], F32, name="last1b", tag="scores02", align_bytes=64))
+        nc.vector.tensor_tensor(last1[1][:], rows[1][:].indirect(offsets(pos[2], halves[1])), t2_wide[:, halves[1]], ADD)
+        w_bf = [keep.tile([P, P, PACK], BF16, name="w_bf0", tag="scores03", align_bytes=64), reuse.tile([P, P, PACK], BF16, name="w_bf1", offset=16384 + 2048, align_bytes=64)]
+        nc.vector.tensor_copy(*rounding(w_bf[0], 0))
+        three = [keep.tile([P, S], F32, name=f"three{h}") for h in range(H)]
+        nc.vector.tensor_tensor(three[0][:], back0[:], last0[:], MAX)
+        w_codes = [reuse.tile([P, P], U32, name="w_codes0", offset=10240, align_bytes=64), keep.tile([P, P], U32, name="w_codes1", align_bytes=64)]
+        quantise(0, w_bf[0])
+
+        picked10 = reuse.tile([P, S], F32, name="picked10", offset=2112)
         pick(picked10[:], 1, 0, whole)
-        bank10 = turn(picked10[:], "turned10", "b0")
-        picked11 = [reuse.tile([P, S // 2], F32, name="picked11a", offset=7488), reuse.tile([P, S // 2], F32, name="picked11b", offset=6464)]
+        bank10 = turn(picked10[:], "turned10", "b3")
+        picked11 = reuse.tile([P, S], F32, name="picked11", offset=6080)
         bank11 = []
-        for i, tag in enumerate(("b1", "b3")):
-            pick(picked11[i][:], 1, 1, halves[i])
-            bank11.append(turn(picked11[i][:], f"turned11{tag}", tag))
+        for cols, tag in zip(halves, ("b0", "b1")):
+            pick(picked11[:, cols], 1, 1, cols)
+            bank11.append(turn(picked11[:, cols], f"turned11{tag}", tag))
         scores1 = with_weight(1, bank10)
 
-        x_codes = keep.tile([P, S], U32, name="x_codes", tag="scores02", align_bytes=64)
+        x_codes = reuse.tile([P, S], U32, name="x_codes", offset=8192, align_bytes=64)
         nc.vector.tensor_copy(x_codes[:], words[:].bitcast(U32).indirect(picks[:]))
-        w_bf = [keep.tile([P, P, PACK], BF16, name="w_bf0", tag="words", align_bytes=64), reuse.tile([P, P, PACK], BF16, name="w_bf1", offset=0, align_bytes=64)]
-        nc.gpsimd.tensor_scalar(w_bf[0][:], w_raw[:, :, 0:P].rearrange("p j n -> p n j"), 1.0, 0.0, MULT, ADD)
         nc.scalar.copy(*rounding(w_bf[1], 1))
-        two1 = keep.tile([P, S], F32, name="two1")
-        three = [keep.tile([P, S], F32, name=f"three{h}") for h in range(H)]
-        res = [keep.tile([P, S], F32, name="res0", tag="scores12", align_bytes=64), keep.tile([P, S], F32, name="res1")]
-        nc.vector.tensor_tensor(three[0][:], back0[:], last0[:], MAX)
-        larger(two1[:, halves[0]], bank11[0], scores1, 0)
-        back1 = [turn(two1[:, halves[0]], "back10", "b4")]
-        quantise(0, w_bf[0])
         y0 = product(0, "y0")
-        larger(two1[:, halves[1]], bank11[1], scores1, 1)
-        back1.append(turn(two1[:, halves[1]], "back11", "b5"))
+        two1 = reuse.tile([P, S], F32, name="two1", offset=16384)
+        res = [keep.tile([P, S], F32, name="res0", tag="w_raw"), keep.tile([P, S], F32, name="res1")]
+        back1 = []
+        for i, cols in enumerate(halves):
+            larger(two1[:, cols], bank11[i], scores1, i)
+            back1.append(turn(two1[:, cols], f"back1{i}", f"b{4 + i}"))
         quantise(1, w_bf[1])
         y1 = product(1, "b6")
         nc.vector.tensor_tensor(res[0][:], y0[:], three[0][:], ADD)

@@ -27,6 +27,7 @@ SCALE_ROWS = K // 32
 SCALES_AT = P - SCALE_ROWS
 T_ROWS = 2 * B
 T_AT = P - T_ROWS
+FUSED = 3 * P
 
 
 def tile_picked_ycrf_vit_p_kernel(tc, x_words, x_scales, w1, alpha, trans, offs, pos1, pos2, pos3, out):
@@ -41,7 +42,7 @@ def tile_picked_ycrf_vit_p_kernel(tc, x_words, x_scales, w1, alpha, trans, offs,
         rows = [keep.tile([P, U], F32, name=f"alpha{h}") for h in range(H)]
         words = reuse.tile([P, T], I32, name="words", offset=16384)
         scales = keep.tile([P, T], U8, name="scales")
-        w_raw = keep.tile([P, PACK, N], F32, name="w_raw", tag="w_raw")
+        w_raw = [keep.tile([P, PACK, P], F32, name=f"w_raw{h}", tag=f"w_raw{h}") for h in range(H)]
         w_scales = [keep.tile([P, P], U8, name=f"w_scales{h}", align_bytes=64) for h in range(H)]
         x_sc = keep.tile([P, S], U8, name="x_sc", align_bytes=64)
         x_rows = keep.tile([P, S], U8, name="x_rows", align_bytes=64)
@@ -65,8 +66,10 @@ def tile_picked_ycrf_vit_p_kernel(tc, x_words, x_scales, w1, alpha, trans, offs,
         nc.sync.dma_start(t_rows[T_AT:P, :], trans[0:2, 0, :].rearrange("d (b j) -> d b j", b=B))
         nc.sync.dma_start(t2_wide[:], trans[2])
         nc.sync.dma_start(rows[1][:], alpha[P : 2 * P, :])
-        nc.sync.dma_start(w_raw[:], w1.rearrange("(p j) n -> p j n", j=PACK))
+        w_rows = w1.rearrange("(p j) n -> p j n", j=PACK)
+        nc.sync.dma_start(w_raw[0][:], w_rows[:, :, 0:P])
         nc.sync.dma_start(words[:], x_words[0].rearrange("p n t -> p (n t)").bitcast(I32))
+        nc.sync.dma_start(w_raw[1][:], w_rows[:, :, P:N])
 
         halves = (slice(0, S // 2), slice(S // 2, S))
         whole = slice(0, S)
@@ -94,14 +97,12 @@ def tile_picked_ycrf_vit_p_kernel(tc, x_words, x_scales, w1, alpha, trans, offs,
                 block = slice(b * P, (b + 1) * P)
                 nc.vector.scalar_tensor_tensor(dst[:, block], bank[:, block], t_cols[:, 1, 2 * i + b : 2 * i + b + 1], scores[2 * i + b][:], ADD, MAX)
 
-        def product(h, tag):
-            bank = psum.tile([P, S], F32, name=f"y{h}", tag=tag)
-            nc.tensor.matmul_mx(out=bank[:], lhsT=w_codes[h][:].bitcast(FP8X4), lhsT_scale=w_scales[h][:],
-                                rhs=x_codes[:].bitcast(FP8X4), rhs_scale=x_sc[:], start=True, stop=True)
-            return bank
+        def product(bank, h, cols):
+            nc.tensor.matmul_mx(out=bank[:, cols], lhsT=w_codes[h][:].bitcast(FP8X4), lhsT_scale=w_scales[h][:],
+                                rhs=x_codes[:, cols].bitcast(FP8X4), rhs_scale=x_sc[:, cols], start=True, stop=True)
 
         def rounding(w_bf, h):
-            return w_bf[:].rearrange("p (c i) j -> p c j i", i=PACK), w_raw[:, :, h * P : (h + 1) * P].rearrange("p j (c i) -> p c j i", i=PACK)
+            return w_bf[:].rearrange("p (c i) j -> p c j i", i=PACK), w_raw[h][:].rearrange("p j (c i) -> p c j i", i=PACK)
 
         def quantise(h, w_bf):
             nc.vector.quantize_mx(out=w_codes[h][:].bitcast(FP8X4), scales=w_scales[h][:], in_=w_bf[:].rearrange("p n j -> p (n j)"))
@@ -129,23 +130,23 @@ def tile_picked_ycrf_vit_p_kernel(tc, x_words, x_scales, w1, alpha, trans, offs,
             bank01.append(turn(picked01[:, cols], f"turned01{tag}", tag))
         t_cols = keep.tile([P, 2, B], F32, name="t_cols", tag="picked00a")
         nc.scalar.copy(t_cols[:].rearrange("p d b -> p (d b)"), t_bank[:, T_AT:P])
-        last0 = keep.tile([P, S], F32, name="last0")
-        nc.vector.tensor_tensor(last0[:], rows[0][:].indirect(pos[2][:]), t2_wide[:], ADD)
+        last = [keep.tile([P, S], F32, name=f"last{h}") for h in range(H)]
+        nc.vector.tensor_tensor(last[0][:], rows[0][:].indirect(pos[2][:]), t2_wide[:], ADD)
         scores0 = with_weight(0, bank00)
-        last1 = [keep.tile([P, S // 2], F32, name="last1a")]
-        nc.vector.tensor_tensor(last1[0][:], rows[1][:].indirect(offsets(pos[2], halves[0])), t2_wide[:, halves[0]], ADD)
-        two0 = reuse.tile([P, S], F32, name="two0", offset=9216)
-        for i, cols in enumerate(halves):
-            larger(two0[:, cols], bank01[i], scores0, i)
-        back0 = turn(two0[:], "back0", "b2")
-        last1.append(keep.tile([P, S // 2], F32, name="last1b", tag="scores02", align_bytes=64))
-        nc.vector.tensor_tensor(last1[1][:], rows[1][:].indirect(offsets(pos[2], halves[1])), t2_wide[:, halves[1]], ADD)
-        w_bf = [keep.tile([P, P, PACK], BF16, name="w_bf0", tag="scores03", align_bytes=64), reuse.tile([P, P, PACK], BF16, name="w_bf1", offset=16384 + 2048, align_bytes=64)]
+        fused, rest = slice(0, FUSED), slice(FUSED, S)
+        nc.vector.tensor_tensor(last[1][:, fused], rows[1][:].indirect(offsets(pos[2], fused)), t2_wide[:, fused], ADD)
+        two0 = [reuse.tile([P, S // 2], F32, name=f"two0{i}", offset=9216 + 1024 * i) for i in range(2)]
+        back0 = []
+        for i, tag in enumerate(("b2", "b4")):
+            larger(two0[i], bank01[i], scores0, i)
+            back0.append(turn(two0[i][:], f"back0{i}", tag))
+        w_bf = [keep.tile([P, P, PACK], BF16, name="w_bf0", tag="scores02", align_bytes=64), reuse.tile([P, P, PACK], BF16, name="w_bf1", offset=2112, align_bytes=64)]
         nc.vector.tensor_copy(*rounding(w_bf[0], 0))
         three = [keep.tile([P, S], F32, name=f"three{h}") for h in range(H)]
-        nc.vector.tensor_tensor(three[0][:], back0[:], last0[:], MAX)
-        w_codes = [reuse.tile([P, P], U32, name="w_codes0", offset=10240, align_bytes=64), keep.tile([P, P], U32, name="w_codes1", align_bytes=64)]
+        nc.vector.tensor_tensor(three[0][:, halves[0]], back0[0][:], last[0][:, halves[0]], MAX)
+        w_codes = [reuse.tile([P, P], U32, name="w_codes0", offset=9216, align_bytes=64), keep.tile([P, P], U32, name="w_codes1", align_bytes=64)]
         quantise(0, w_bf[0])
+        nc.vector.tensor_tensor(three[0][:, halves[1]], back0[1][:], last[0][:, halves[1]], MAX)
 
         picked10 = reuse.tile([P, S], F32, name="picked10", offset=2112)
         pick(picked10[:], 1, 0, whole)
@@ -157,22 +158,28 @@ def tile_picked_ycrf_vit_p_kernel(tc, x_words, x_scales, w1, alpha, trans, offs,
             bank11.append(turn(picked11[:, cols], f"turned11{tag}", tag))
         scores1 = with_weight(1, bank10)
 
-        x_codes = reuse.tile([P, S], U32, name="x_codes", offset=8192, align_bytes=64)
-        nc.vector.tensor_copy(x_codes[:], words[:].bitcast(U32).indirect(picks[:]))
         nc.scalar.copy(*rounding(w_bf[1], 1))
-        y0 = product(0, "y0")
+        picked12 = reuse.tile([P, S - FUSED], F32, name="picked12", offset=2112 + 1024)
+        pick(picked12[:], 1, 2, rest)
+        nc.gpsimd.tensor_tensor(last[1][:, rest], picked12[:], t2_wide[:, rest], ADD)
+
+        x_codes = reuse.tile([P, S], U32, name="x_codes", offset=10240, align_bytes=64)
+        y = [psum.tile([P, S], F32, name="y0", tag="y0"), psum.tile([P, S], F32, name="y1", tag="b6")]
+        for cols in halves:
+            nc.vector.tensor_copy(x_codes[:, cols], words[:].bitcast(U32).indirect(offsets(picks, cols)))
+            product(y[0], 0, cols)
         two1 = reuse.tile([P, S], F32, name="two1", offset=16384)
-        res = [keep.tile([P, S], F32, name="res0", tag="w_raw"), keep.tile([P, S], F32, name="res1")]
+        res = [keep.tile([P, S], F32, name="res0", tag="w_raw1"), keep.tile([P, S], F32, name="res1")]
         back1 = []
-        for i, cols in enumerate(halves):
+        for i, (cols, tag) in enumerate(zip(halves, ("b2", "b5"))):
             larger(two1[:, cols], bank11[i], scores1, i)
-            back1.append(turn(two1[:, cols], f"back1{i}", f"b{4 + i}"))
+            back1.append(turn(two1[:, cols], f"back1{i}", tag))
         quantise(1, w_bf[1])
-        y1 = product(1, "b6")
-        nc.vector.tensor_tensor(res[0][:], y0[:], three[0][:], ADD)
+        product(y[1], 1, whole)
+        nc.vector.tensor_tensor(res[0][:], y[0][:], three[0][:], ADD)
         nc.sync.dma_start(out[0:P, :], res[0][:])
         for i, cols in enumerate(halves):
-            nc.vector.tensor_tensor(three[1][:, cols], back1[i][:], last1[i][:], MAX)
+            nc.vector.tensor_tensor(three[1][:, cols], back1[i][:], last[1][:, cols], MAX)
         for cols in halves:
-            nc.vector.tensor_tensor(res[1][:, cols], y1[:, cols], three[1][:, cols], ADD)
+            nc.vector.tensor_tensor(res[1][:, cols], y[1][:, cols], three[1][:, cols], ADD)
             nc.sync.dma_start(out[P:N, cols], res[1][:, cols])

@@ -27,7 +27,6 @@ SCALE_ROWS = K // 32
 SCALES_AT = P - SCALE_ROWS
 T_ROWS = 2 * B
 T_AT = P - T_ROWS
-FUSED = 3 * P
 
 
 def tile_picked_ycrf_vit_p_kernel(tc, x_words, x_scales, w1, alpha, trans, offs, pos1, pos2, pos3, out):
@@ -98,7 +97,7 @@ def tile_picked_ycrf_vit_p_kernel(tc, x_words, x_scales, w1, alpha, trans, offs,
                 nc.vector.scalar_tensor_tensor(dst[:, block], bank[:, block], t_cols[:, 1, 2 * i + b : 2 * i + b + 1], scores[2 * i + b][:], ADD, MAX)
 
         def product(bank, h, cols):
-            nc.tensor.matmul_mx(out=bank[:, cols], lhsT=w_codes[h][:].bitcast(FP8X4), lhsT_scale=w_scales[h][:],
+            nc.tensor.matmul_mx(out=bank, lhsT=w_codes[h][:].bitcast(FP8X4), lhsT_scale=w_scales[h][:],
                                 rhs=x_codes[:, cols].bitcast(FP8X4), rhs_scale=x_sc[:, cols], start=True, stop=True)
 
         def rounding(w_bf, h):
@@ -133,8 +132,7 @@ def tile_picked_ycrf_vit_p_kernel(tc, x_words, x_scales, w1, alpha, trans, offs,
         last = [keep.tile([P, S], F32, name=f"last{h}") for h in range(H)]
         nc.vector.tensor_tensor(last[0][:], rows[0][:].indirect(pos[2][:]), t2_wide[:], ADD)
         scores0 = with_weight(0, bank00)
-        fused, rest = slice(0, FUSED), slice(FUSED, S)
-        nc.vector.tensor_tensor(last[1][:, fused], rows[1][:].indirect(offsets(pos[2], fused)), t2_wide[:, fused], ADD)
+        nc.vector.tensor_tensor(last[1][:], rows[1][:].indirect(pos[2][:]), t2_wide[:], ADD)
         two0 = [reuse.tile([P, S // 2], F32, name=f"two0{i}", offset=9216 + 1024 * i) for i in range(2)]
         back0 = []
         for i, tag in enumerate(("b2", "b4")):
@@ -159,27 +157,31 @@ def tile_picked_ycrf_vit_p_kernel(tc, x_words, x_scales, w1, alpha, trans, offs,
         scores1 = with_weight(1, bank10)
 
         nc.scalar.copy(*rounding(w_bf[1], 1))
-        picked12 = reuse.tile([P, S - FUSED], F32, name="picked12", offset=2112 + 1024)
-        pick(picked12[:], 1, 2, rest)
-        nc.gpsimd.tensor_tensor(last[1][:, rest], picked12[:], t2_wide[:, rest], ADD)
 
         x_codes = reuse.tile([P, S], U32, name="x_codes", offset=10240, align_bytes=64)
-        y = [psum.tile([P, S], F32, name="y0", tag="y0"), psum.tile([P, S], F32, name="y1", tag="b6")]
-        for cols in halves:
+        y0 = [psum.tile([P, S // 2], F32, name=f"y0{i}", tag=tag) for i, tag in enumerate(("y0", "b4"))]
+        y1 = [psum.tile([P, S // 2], F32, name=f"y1{i}", tag=tag) for i, tag in enumerate(("b6", "b3"))]
+        for i, cols in enumerate(halves):
             nc.vector.tensor_copy(x_codes[:, cols], words[:].bitcast(U32).indirect(offsets(picks, cols)))
-            product(y[0], 0, cols)
+            product(y0[i][:], 0, cols)
         two1 = reuse.tile([P, S], F32, name="two1", offset=16384)
-        res = [keep.tile([P, S], F32, name="res0", tag="w_raw1"), keep.tile([P, S], F32, name="res1")]
+        res0 = [keep.tile([P, S // 2], F32, name="res0a", tag="w_raw1"), reuse.tile([P, S // 2], F32, name="res0b", offset=2112)]
+        res1 = keep.tile([P, S], F32, name="res1")
         back1 = []
         for i, (cols, tag) in enumerate(zip(halves, ("b2", "b5"))):
             larger(two1[:, cols], bank11[i], scores1, i)
             back1.append(turn(two1[:, cols], f"back1{i}", tag))
         quantise(1, w_bf[1])
-        product(y[1], 1, whole)
-        nc.vector.tensor_tensor(res[0][:], y[0][:], three[0][:], ADD)
-        nc.sync.dma_start(out[0:P, :], res[0][:])
+        for i, cols in enumerate(halves):
+            product(y1[i][:], 1, cols)
+        y0_copy = keep.tile([P, S // 2], F32, name="y0_copy")
+        nc.scalar.copy(y0_copy[:], y0[0][:])
+        nc.gpsimd.tensor_tensor(res0[1][:], y0_copy[:], three[0][:, halves[0]], ADD)
+        nc.vector.tensor_tensor(res0[0][:], y0[1][:], three[0][:, halves[1]], ADD)
+        nc.sync.dma_start(out[0:P, halves[1]], res0[0][:])
+        nc.sync.dma_start(out[0:P, halves[0]], res0[1][:])
         for i, cols in enumerate(halves):
             nc.vector.tensor_tensor(three[1][:, cols], back1[i][:], last[1][:, cols], MAX)
-        for cols in halves:
-            nc.vector.tensor_tensor(res[1][:, cols], y[1][:, cols], three[1][:, cols], ADD)
-            nc.sync.dma_start(out[P:N, cols], res[1][:, cols])
+        for i, cols in enumerate(halves):
+            nc.vector.tensor_tensor(res1[:, cols], y1[i][:], three[1][:, cols], ADD)
+            nc.sync.dma_start(out[P:N, cols], res1[:, cols])

@@ -57,12 +57,12 @@ def tile_picked_ycrf_vit_p_kernel(tc, x_words, x_scales, w1, alpha, trans, offs,
         nc.scalar.copy(ident[:], ident_bf[:])
 
         nc.sync.dma_start(picks[:], offs)
-        nc.sync.dma_start(scales[SCALES_AT:P, :].bitcast(I32), x_scales[0].bitcast(I32))
+        nc.scalar.dma_start(scales[SCALES_AT:P, :].bitcast(I32), x_scales[0].bitcast(I32))
         nc.sync.dma_start(rows[0][:], alpha[0:P, :])
+        nc.scalar.dma_start(t_rows[T_AT:P, :], trans[0:2, 0, :].rearrange("d (b j) -> d b j", b=B))
         nc.sync.dma_start(pos[0][:], pos1)
         nc.sync.dma_start(pos[1][:], pos2)
         nc.sync.dma_start(pos[2][:], pos3)
-        nc.sync.dma_start(t_rows[T_AT:P, :], trans[0:2, 0, :].rearrange("d (b j) -> d b j", b=B))
         nc.sync.dma_start(t2_wide[:], trans[2])
         nc.sync.dma_start(rows[1][:], alpha[P : 2 * P, :])
         w_rows = w1.rearrange("(p j) n -> p j n", j=PACK)

@@ -48,7 +48,7 @@ def tile_picked_ycrf_vit_p_kernel(tc, x_words, x_scales, w1, alpha, trans, offs,
         ident = keep.tile([P, P], F32, name="ident")
         t_rows = keep.tile([P, P], F32, name="t_rows")
         ident_bf = reuse.tile([P, P], BF16, name="ident_bf", offset=4096 - 128)
-        t2_wide = keep.tile([P, S], F32, name="t2_wide")
+        t2_wide = keep.tile([P, S], F32, name="t2_wide", tag="t2_wide", align_bytes=64)
 
         make_identity(nc, ident_bf[:])
         nc.gpsimd.memset(t_rows[0:T_AT, :], 0.0)
@@ -138,8 +138,8 @@ def tile_picked_ycrf_vit_p_kernel(tc, x_words, x_scales, w1, alpha, trans, offs,
         for i, tag in enumerate(("b2", "b4")):
             larger(two0[i], bank01[i], scores0, i)
             back0.append(turn(two0[i][:], f"back0{i}", tag))
-        w_bf = [keep.tile([P, P, PACK], BF16, name="w_bf0", tag="scores02", align_bytes=64), reuse.tile([P, P, PACK], BF16, name="w_bf1", offset=2112, align_bytes=64)]
-        nc.vector.tensor_copy(*rounding(w_bf[0], 0))
+        w_bf = [keep.tile([P, P, PACK], BF16, name="w_bf0", tag="t2_wide", align_bytes=64), reuse.tile([P, P, PACK], BF16, name="w_bf1", offset=2112, align_bytes=64)]
+        nc.gpsimd.tensor_scalar(w_bf[0][:], w_raw[0][:].rearrange("p j n -> p n j"), 1.0, 0.0, MULT, ADD)
         three = [keep.tile([P, S], F32, name=f"three{h}") for h in range(H)]
         nc.vector.tensor_tensor(three[0][:, halves[0]], back0[0][:], last[0][:, halves[0]], MAX)
         w_codes = [reuse.tile([P, P], U32, name="w_codes0", offset=9216, align_bytes=64), keep.tile([P, P], U32, name="w_codes1", align_bytes=64)]

@@ -138,6 +138,9 @@ def tile_picked_ycrf_vit_p_kernel(tc, x_words, x_scales, w1, alpha, trans, offs,
         for i, tag in enumerate(("b2", "b4")):
             larger(two0[i], bank01[i], scores0, i)
             back0.append(turn(two0[i][:], f"back0{i}", tag))
+        third, fourth = slice(2 * P, 3 * P), slice(3 * P, S)
+        picked11v = keep.tile([P, P], F32, name="picked11v", tag="scores02", align_bytes=64)
+        nc.vector.tensor_copy(picked11v[:], rows[1][:].indirect(offsets(pos[1], fourth)))
         w_bf = [keep.tile([P, P, PACK], BF16, name="w_bf0", tag="t2_wide", align_bytes=64), reuse.tile([P, P, PACK], BF16, name="w_bf1", offset=2112, align_bytes=64)]
         nc.gpsimd.tensor_scalar(w_bf[0][:], w_raw[0][:].rearrange("p j n -> p n j"), 1.0, 0.0, MULT, ADD)
         three = [keep.tile([P, S], F32, name=f"three{h}") for h in range(H)]
@@ -151,9 +154,12 @@ def tile_picked_ycrf_vit_p_kernel(tc, x_words, x_scales, w1, alpha, trans, offs,
         bank10 = turn(picked10[:], "turned10", "b3")
         picked11 = reuse.tile([P, S], F32, name="picked11", offset=6080)
         bank11 = []
-        for cols, tag in zip(halves, ("b0", "b1")):
-            pick(picked11[:, cols], 1, 1, cols)
-            bank11.append(turn(picked11[:, cols], f"turned11{tag}", tag))
+        pick(picked11[:, halves[0]], 1, 1, halves[0])
+        bank11.append(turn(picked11[:, halves[0]], "turned11a", "b0"))
+        pick(picked11[:, third], 1, 1, third)
+        bank11.append(psum.tile([P, S // 2], F32, name="turned11b", tag="b1"))
+        turn_into(bank11[1], picked11v[:], slice(P, 2 * P))
+        turn_into(bank11[1], picked11[:, third], slice(0, P))
         scores1 = with_weight(1, bank10)
 
         nc.scalar.copy(*rounding(w_bf[1], 1))

@@ -129,7 +129,7 @@ def tile_picked_ycrf_vit_p_kernel(tc, x_words, x_scales, w1, alpha, trans, offs,
             bank01.append(turn(picked01[:, cols], f"turned01{tag}", tag))
         t_cols = keep.tile([P, 2, B], F32, name="t_cols", tag="picked00a")
         nc.scalar.copy(t_cols[:].rearrange("p d b -> p (d b)"), t_bank[:, T_AT:P])
-        last = [keep.tile([P, S], F32, name=f"last{h}") for h in range(H)]
+        last = [keep.tile([P, S], F32, name=f"last{h}", tag=f"last{h}") for h in range(H)]
         nc.vector.tensor_tensor(last[0][:], rows[0][:].indirect(pos[2][:]), t2_wide[:], ADD)
         scores0 = with_weight(0, bank00)
         nc.vector.tensor_tensor(last[1][:], rows[1][:].indirect(pos[2][:]), t2_wide[:], ADD)
@@ -170,7 +170,7 @@ def tile_picked_ycrf_vit_p_kernel(tc, x_words, x_scales, w1, alpha, trans, offs,
         for i, cols in enumerate(halves):
             nc.vector.tensor_copy(x_codes[:, cols], words[:].bitcast(U32).indirect(offsets(picks, cols)))
             product(y0[i][:], 0, cols)
-        two1 = reuse.tile([P, S], F32, name="two1", offset=16384)
+        two1 = keep.tile([P, S], F32, name="two1", tag="last0")
         res0 = [keep.tile([P, S // 2], F32, name="res0a", tag="w_raw1"), reuse.tile([P, S // 2], F32, name="res0b", offset=2112)]
         res1 = keep.tile([P, S], F32, name="res1")
         back1 = []

@@ -40,13 +40,13 @@ def tile_picked_ycrf_vit_p_kernel(tc, x_words, x_scales, w1, alpha, trans, offs,
         picks = keep.tile([P, S // 16], U16, name="picks")
         rows = [keep.tile([P, U], F32, name=f"alpha{h}") for h in range(H)]
         words = reuse.tile([P, T], I32, name="words", offset=16384)
-        scales = keep.tile([P, T], U8, name="scales")
+        scales = keep.tile([P, T], U8, name="scales", tag="scales")
         w_raw = [keep.tile([P, PACK, P], F32, name=f"w_raw{h}", tag=f"w_raw{h}") for h in range(H)]
         w_scales = [keep.tile([P, P], U8, name=f"w_scales{h}", align_bytes=64) for h in range(H)]
         x_sc = keep.tile([P, S], U8, name="x_sc", align_bytes=64)
         x_rows = keep.tile([P, S], U8, name="x_rows", align_bytes=64)
         ident = keep.tile([P, P], F32, name="ident")
-        t_rows = keep.tile([P, P], F32, name="t_rows")
+        t_rows = reuse.tile([P, P], F32, name="t_rows", offset=28672 - 256)
         ident_bf = reuse.tile([P, P], BF16, name="ident_bf", offset=4096 - 128)
         t2_wide = keep.tile([P, S], F32, name="t2_wide", tag="t2_wide", align_bytes=64)
 
@@ -120,6 +120,8 @@ def tile_picked_ycrf_vit_p_kernel(tc, x_words, x_scales, w1, alpha, trans, offs,
         pick(picked00[1][:], 0, 0, halves[1])
         t_bank = psum.tile([P, P], F32, name="t_bank", tag="y0")
         nc.tensor.transpose(t_bank[:], t_rows[:], ident[:])
+        t_cols = keep.tile([P, 2, B], F32, name="t_cols", tag="scales")
+        nc.vector.tensor_copy(t_cols[:].rearrange("p d b -> p (d b)"), t_bank[:, T_AT:P])
         for i, cols in enumerate(halves):
             turn_into(bank00, picked00[i][:], cols)
         picked01 = reuse.tile([P, S], F32, name="picked01", offset=4096)
@@ -127,9 +129,7 @@ def tile_picked_ycrf_vit_p_kernel(tc, x_words, x_scales, w1, alpha, trans, offs,
         for cols, tag in zip(halves, ("b1", "b3")):
             pick(picked01[:, cols], 0, 1, cols)
             bank01.append(turn(picked01[:, cols], f"turned01{tag}", tag))
-        t_cols = keep.tile([P, 2, B], F32, name="t_cols", tag="picked00a")
-        nc.scalar.copy(t_cols[:].rearrange("p d b -> p (d b)"), t_bank[:, T_AT:P])
-        last = [keep.tile([P, S], F32, name=f"last{h}", tag=f"last{h}") for h in range(H)]
+        last = [reuse.tile([P, S], F32, name=f"last{h}", offset=26624 + 2048 * h) for h in range(H)]
         nc.vector.tensor_tensor(last[0][:], rows[0][:].indirect(pos[2][:]), t2_wide[:], ADD)
         scores0 = with_weight(0, bank00)
         nc.vector.tensor_tensor(last[1][:], rows[1][:].indirect(pos[2][:]), t2_wide[:], ADD)
@@ -170,7 +170,7 @@ def tile_picked_ycrf_vit_p_kernel(tc, x_words, x_scales, w1, alpha, trans, offs,
         for i, cols in enumerate(halves):
             nc.vector.tensor_copy(x_codes[:, cols], words[:].bitcast(U32).indirect(offsets(picks, cols)))
             product(y0[i][:], 0, cols)
-        two1 = keep.tile([P, S], F32, name="two1", tag="last0")
+        two1 = reuse.tile([P, S], F32, name="two1", offset=26624)
         res0 = [keep.tile([P, S // 2], F32, name="res0a", tag="w_raw1"), reuse.tile([P, S // 2], F32, name="res0b", offset=2112)]
         res1 = keep.tile([P, S], F32, name="res1")
         back1 = []

from contextlib import ExitStack

import concourse.mybir as mybir
from concourse.masks import make_identity

K, T, S, N, D, U = 512, 2048, 512, 256, 3, 1024
P = 128
PACK = 4
FLOPS = 2 * K * N * S

F32 = mybir.dt.float32
BF16 = mybir.dt.bfloat16
I32 = mybir.dt.int32
U32 = mybir.dt.uint32
U16 = mybir.dt.uint16
U8 = mybir.dt.uint8
FP8X4 = mybir.dt.float8_e4m3fn_x4
ADD = mybir.AluOpType.add
MULT = mybir.AluOpType.mult
MAX = mybir.AluOpType.max
IDENTITY = mybir.ActivationFunctionType.Identity
COPY = mybir.ActivationFunctionType.Copy
B = S // P
H = N // P
QUAD = 32
SCALE_ROWS = K // 32
SCALES_AT = P - SCALE_ROWS
T_ROWS = 2 * B
T_AT = P - T_ROWS


def tile_picked_ycrf_vit_p_kernel(tc, x_words, x_scales, w1, alpha, trans, offs, pos1, pos2, pos3, out):
    nc = tc.nc
    with ExitStack() as ctx:
        keep = ctx.enter_context(tc.tile_pool(name="keep", bufs=1))
        reuse = ctx.enter_context(tc.tile_pool(name="reuse", bufs=1))
        psum = ctx.enter_context(tc.psum_pool(name="psum", bufs=1))

        pos = [keep.tile([P, S // 16], U16, name=f"pos{d}") for d in range(D)]
        picks = keep.tile([P, S // 16], U16, name="picks")
        rows = [keep.tile([P, U], F32, name=f"alpha{h}") for h in range(H)]
        words = reuse.tile([P, T], I32, name="words", offset=16384)
        scales = keep.tile([P, T], U8, name="scales", tag="scales")
        w_raw = [keep.tile([P, PACK, P], F32, name=f"w_raw{h}", tag=f"w_raw{h}") for h in range(H)]
        w_scales = [keep.tile([P, P], U8, name=f"w_scales{h}", align_bytes=64) for h in range(H)]
        x_sc = keep.tile([P, S], U8, name="x_sc", align_bytes=64)
        x_rows = keep.tile([P, S], U8, name="x_rows", align_bytes=64)
        ident = keep.tile([P, P], F32, name="ident")
        t_rows = reuse.tile([P, P], F32, name="t_rows", offset=28672 - 256)
        ident_bf = reuse.tile([P, P], BF16, name="ident_bf", offset=4096 - 128)
        t2_wide = keep.tile([P, S], F32, name="t2_wide", tag="t2_wide", align_bytes=64)

        make_identity(nc, ident_bf[:])
        nc.gpsimd.memset(t_rows[0:T_AT, :], 0.0)
        nc.gpsimd.memset(x_sc[:].bitcast(I32), 0)
        nc.vector.memset(scales[0:SCALES_AT, :].bitcast(I32), 0)
        nc.scalar.copy(ident[:], ident_bf[:])

        nc.sync.dma_start(picks[:], offs)
        nc.scalar.dma_start(scales[SCALES_AT:P, :].bitcast(I32), x_scales[0].bitcast(I32))
        nc.sync.dma_start(rows[0][:], alpha[0:P, :])
        nc.scalar.dma_start(t_rows[T_AT:P, :], trans[0:2, 0, :].rearrange("d (b j) -> d b j", b=B))
        nc.sync.dma_start(pos[0][:], pos1)
        nc.sync.dma_start(pos[1][:], pos2)
        nc.sync.dma_start(pos[2][:], pos3)
        nc.sync.dma_start(t2_wide[:], trans[2])
        nc.sync.dma_start(rows[1][:], alpha[P : 2 * P, :])
        w_rows = w1.rearrange("(p j) n -> p j n", j=PACK)
        nc.sync.dma_start(w_raw[0][:], w_rows[:, :, 0:P])
        nc.sync.dma_start(words[:], x_words[0].rearrange("p n t -> p (n t)").bitcast(I32))
        nc.sync.dma_start(w_raw[1][:], w_rows[:, :, P:N])

        halves = (slice(0, S // 2), slice(S // 2, S))
        whole = slice(0, S)

        def offsets(lst, cols):
            return lst[:, cols.start // 16 : cols.stop // 16]

        def turn(src, name, tag):
            bank = psum.tile([P, src.shape[1]], F32, name=name, tag=tag)
            for b in range(src.shape[1] // P):
                nc.tensor.transpose(bank[:, b * P : (b + 1) * P], src[:, b * P : (b + 1) * P], ident[:])
            return bank

        def pick(dst, h, d, cols):
            nc.scalar.activation(dst, rows[h][:].indirect(offsets(pos[d], cols)), COPY)

        def with_weight(h, bank):
            scores = [keep.tile([P, P], F32, name=f"scores{h}{b}", tag=f"scores{h}{b}", align_bytes=64) for b in range(B)]
            for b in range(B):
                nc.scalar.activation(scores[b][:], bank[:, b * P : (b + 1) * P], IDENTITY, bias=t_cols[:, 0, b : b + 1])
            return scores

        def larger(dst, bank, scores, i):
            for b in range(2):
                block = slice(b * P, (b + 1) * P)
                nc.vector.scalar_tensor_tensor(dst[:, block], bank[:, block], t_cols[:, 1, 2 * i + b : 2 * i + b + 1], scores[2 * i + b][:], ADD, MAX)

        def product(bank, h, cols):
            nc.tensor.matmul_mx(out=bank, lhsT=w_codes[h][:].bitcast(FP8X4), lhsT_scale=w_scales[h][:],
                                rhs=x_codes[:, cols].bitcast(FP8X4), rhs_scale=x_sc[:, cols], start=True, stop=True)

        def rounding(w_bf, h):
            return w_bf[:].rearrange("p (c i) j -> p c j i", i=PACK), w_raw[h][:].rearrange("p j (c i) -> p c j i", i=PACK)

        def quantise(h, w_bf):
            nc.vector.quantize_mx(out=w_codes[h][:].bitcast(FP8X4), scales=w_scales[h][:], in_=w_bf[:].rearrange("p n j -> p (n j)"))

        def turn_into(bank, src, cols):
            for b in range(src.shape[1] // P):
                nc.tensor.transpose(bank[:, cols.start + b * P : cols.start + (b + 1) * P], src[:, b * P : (b + 1) * P], ident[:])

        nc.vector.tensor_copy(x_rows[:], scales[:].indirect(picks[:]))
        for q in range(4):
            nc.sync.dma_start(x_sc[QUAD * q : QUAD * q + 4, :].bitcast(I32), x_rows[SCALES_AT + 4 * q : SCALES_AT + 4 * q + 4, :].bitcast(I32))

        picked00 = [keep.tile([P, S // 2], F32, name="picked00a", tag="picked00a"), reuse.tile([P, S // 2], F32, name="picked00b", offset=3072)]
        bank00 = psum.tile([P, S], F32, name="turned00", tag="b0")
        nc.vector.tensor_copy(picked00[0][:], rows[0][:].indirect(offsets(pos[0], halves[0])))
        pick(picked00[1][:], 0, 0, halves[1])
        t_bank = psum.tile([P, P], F32, name="t_bank", tag="y0")
        nc.tensor.transpose(t_bank[:], t_rows[:], ident[:])
        t_cols = keep.tile([P, 2, B], F32, name="t_cols", tag="scales")
        nc.vector.tensor_copy(t_cols[:].rearrange("p d b -> p (d b)"), t_bank[:, T_AT:P])
        for i, cols in enumerate(halves):
            turn_into(bank00, picked00[i][:], cols)
        picked01 = reuse.tile([P, S], F32, name="picked01", offset=4096)
        bank01 = []
        for cols, tag in zip(halves, ("b1", "b3")):
            pick(picked01[:, cols], 0, 1, cols)
            bank01.append(turn(picked01[:, cols], f"turned01{tag}", tag))
        last = [reuse.tile([P, S], F32, name=f"last{h}", offset=26624 + 2048 * h) for h in range(H)]
        nc.vector.tensor_tensor(last[0][:], rows[0][:].indirect(pos[2][:]), t2_wide[:], ADD)
        scores0 = with_weight(0, bank00)
        nc.vector.tensor_tensor(last[1][:], rows[1][:].indirect(pos[2][:]), t2_wide[:], ADD)
        two0 = [reuse.tile([P, S // 2], F32, name=f"two0{i}", offset=9216 + 1024 * i) for i in range(2)]
        back0 = []
        for i, tag in enumerate(("b2", "b4")):
            larger(two0[i], bank01[i], scores0, i)
            back0.append(turn(two0[i][:], f"back0{i}", tag))
        third, fourth = slice(2 * P, 3 * P), slice(3 * P, S)
        picked11v = keep.tile([P, P], F32, name="picked11v", tag="scores02", align_bytes=64)
        nc.vector.tensor_copy(picked11v[:], rows[1][:].indirect(offsets(pos[1], fourth)))
        w_bf = [keep.tile([P, P, PACK], BF16, name="w_bf0", tag="t2_wide", align_bytes=64), reuse.tile([P, P, PACK], BF16, name="w_bf1", offset=2112, align_bytes=64)]
        nc.gpsimd.tensor_scalar(w_bf[0][:], w_raw[0][:].rearrange("p j n -> p n j"), 1.0, 0.0, MULT, ADD)
        three = [keep.tile([P, S], F32, name=f"three{h}") for h in range(H)]
        nc.vector.tensor_tensor(three[0][:, halves[0]], back0[0][:], last[0][:, halves[0]], MAX)
        w_codes = [reuse.tile([P, P], U32, name="w_codes0", offset=9216, align_bytes=64), keep.tile([P, P], U32, name="w_codes1", align_bytes=64)]
        quantise(0, w_bf[0])
        nc.vector.tensor_tensor(three[0][:, halves[1]], back0[1][:], last[0][:, halves[1]], MAX)

        picked10 = reuse.tile([P, S], F32, name="picked10", offset=2112)
        pick(picked10[:], 1, 0, whole)
        bank10 = turn(picked10[:], "turned10", "b3")
        picked11 = reuse.tile([P, S], F32, name="picked11", offset=6080)
        bank11 = []
        pick(picked11[:, halves[0]], 1, 1, halves[0])
        bank11.append(turn(picked11[:, halves[0]], "turned11a", "b0"))
        pick(picked11[:, third], 1, 1, third)
        bank11.append(psum.tile([P, S // 2], F32, name="turned11b", tag="b1"))
        turn_into(bank11[1], picked11v[:], slice(P, 2 * P))
        turn_into(bank11[1], picked11[:, third], slice(0, P))
        scores1 = with_weight(1, bank10)

        nc.scalar.copy(*rounding(w_bf[1], 1))

        x_codes = reuse.tile([P, S], U32, name="x_codes", offset=10240, align_bytes=64)
        y0 = [psum.tile([P, S // 2], F32, name=f"y0{i}", tag=tag) for i, tag in enumerate(("y0", "b4"))]
        y1 = [psum.tile([P, S // 2], F32, name=f"y1{i}", tag=tag) for i, tag in enumerate(("b6", "b3"))]
        for i, cols in enumerate(halves):
            nc.vector.tensor_copy(x_codes[:, cols], words[:].bitcast(U32).indirect(offsets(picks, cols)))
            product(y0[i][:], 0, cols)
        two1 = reuse.tile([P, S], F32, name="two1", offset=26624)
        res0 = [keep.tile([P, S // 2], F32, name="res0a", tag="w_raw1"), reuse.tile([P, S // 2], F32, name="res0b", offset=2112)]
        res1 = keep.tile([P, S], F32, name="res1")
        back1 = []
        for i, (cols, tag) in enumerate(zip(halves, ("b2", "b5"))):
            larger(two1[:, cols], bank11[i], scores1, i)
            back1.append(turn(two1[:, cols], f"back1{i}", tag))
        quantise(1, w_bf[1])
        for i, cols in enumerate(halves):
            product(y1[i][:], 1, cols)
        y0_copy = keep.tile([P, S // 2], F32, name="y0_copy")
        nc.scalar.copy(y0_copy[:], y0[0][:])
        nc.gpsimd.tensor_tensor(res0[1][:], y0_copy[:], three[0][:, halves[0]], ADD)
        nc.vector.tensor_tensor(res0[0][:], y0[1][:], three[0][:, halves[1]], ADD)
        nc.sync.dma_start(out[0:P, halves[1]], res0[0][:])
        nc.sync.dma_start(out[0:P, halves[0]], res0[1][:])
        for i, cols in enumerate(halves):
            nc.vector.tensor_tensor(three[1][:, cols], back1[i][:], last[1][:, cols], MAX)
        for i, cols in enumerate(halves):
            nc.vector.tensor_tensor(res1[:, cols], y1[i][:], three[1][:, cols], ADD)
            nc.sync.dma_start(out[P:N, cols], res1[:, cols])
